import numpy as np
import ml_dtypes


def mxq(x, axis, fmt="e4m3"):
    dtype, down = {"e4m3": (ml_dtypes.float8_e4m3fn, 7), "e5m2": (ml_dtypes.float8_e5m2, 14)}[fmt]
    v = np.moveaxis(np.asarray(x, np.float32).astype(ml_dtypes.bfloat16).astype(np.float64), axis, -1)
    blocks = v.reshape(v.shape[:-1] + (-1, 32))
    amax = np.abs(blocks).max(-1, keepdims=True)
    byte = np.maximum(np.where(amax > 0, np.frexp(amax)[1] - 1 + 127, 0) - down, 1)
    scale = np.exp2(byte - 127.0)
    codes = (blocks / scale).astype(np.float32).astype(dtype).astype(np.float64)
    return np.moveaxis((codes * scale).reshape(v.shape), -1, axis)


WIDE = False


def mx_kscale(k):
    if not WIDE:
        return np.ones(k)
    levels = np.array([10, -10, 5, -5, 0])
    if k % 512:
        return np.exp2(np.random.permutation(np.resize(levels, k // 32))).repeat(32)
    a = np.empty((k // 512, 16))
    for p in range(k // 512):
        a[p, :8] = np.random.permutation(np.resize(levels, 8))
        for g in range(8):
            far = levels[np.abs(levels - a[p, g]) >= 10]
            a[p, g + 8] = far[np.random.randint(len(far))]
    return np.exp2(a.ravel()).repeat(32)


def f64(x):
    return np.asarray(x).astype(np.float64)


def striped(idx):
    return np.tile(np.asarray(idx).reshape(-1, 16).T, (8, 1)).astype(np.uint16)


def unstriped(offs):
    return offs[:16].T.reshape(-1).astype(np.int64)


B, N, T, D, DV, NQ = 1, 512, 1024, 512, 256, 128
SINKS = 64


def setup_inputs():
    n = np.random.standard_normal
    head = np.random.randint(0, T // B)
    ring = T // B
    sinks = np.arange(SINKS)
    win = SINKS + (head + np.arange(N - SINKS)) % (ring - SINKS)
    idx = np.concatenate([b * ring + np.concatenate([sinks, win]) for b in range(B)])
    s = mx_kscale(D)[:, None]
    u = np.ones(T)
    u[idx] = mx_kscale(B * N)
    r = np.random.uniform(0.5, 2.0, T)
    k = n((D, T)) / s
    v = n((DV, T)) / (u * r)
    when = np.zeros(T)
    when[idx] = np.sort(np.random.permutation(2 * N)[:B * N])
    return {
        "qT": (n((B, D, NQ)) * s * (0.60 / np.sqrt(D))).astype(np.float32),
        "kT": k.astype(np.float32),
        "vT": v.astype(np.float32),
        "vs": np.tile(u * r, (128, 1)).astype(np.float32),
        "pos": np.tile(when, (128, 1)).astype(np.float32),
        "slope": np.exp2(-np.random.randint(8, 13, (B, NQ, 1))).astype(np.float32),
        "offs": striped(idx),
    }


def reference(qT, kT, vT, vs, pos, slope, offs):
    idx = unstriped(offs)
    k = f64(kT)
    v = f64(vT)
    pick = lambda x: x[:, idx].reshape(x.shape[0], B, N).transpose(1, 0, 2)
    q = f64(qT)
    score = mxq(q, 1, "e4m3").transpose(0, 2, 1) @ mxq(pick(k), 1, "e4m3")
    score = score + f64(slope) * pick(f64(pos))[:, :1, :]
    m = score.max(-1, keepdims=True)
    p = np.exp(score - m)
    total = p.sum(-1, keepdims=True)
    w = p * pick(f64(vs))[:, :1, :]
    y = mxq(w, 2, "e4m3") @ mxq(pick(v).transpose(0, 2, 1), 1, "e4m3")
    y = y / total
    return y

@@ -1,0 +1,168 @@
+from contextlib import ExitStack
+
+import concourse.mybir as mybir
+from concourse.masks import make_identity
+
+NQ, D, N, T, DV = 128, 512, 512, 1024, 256
+P = 128
+FLOPS = 2 * NQ * N * (D + DV)
+
+F32 = mybir.dt.float32
+BF16 = mybir.dt.bfloat16
+U32 = mybir.dt.uint32
+U16 = mybir.dt.uint16
+U8 = mybir.dt.uint8
+FP8X4 = mybir.dt.float8_e4m3fn_x4
+ADD, MULT, MAX = mybir.AluOpType.add, mybir.AluOpType.mult, mybir.AluOpType.max
+EXP = mybir.ActivationFunctionType.Exp
+COPY = mybir.ActivationFunctionType.Copy
+X = mybir.AxisListType.X
+
+
+def tile_attend_ring_alibi_kernel(tc, qT, kT, vT, vs, pos, slope, offs, out):
+    nc = tc.nc
+    with ExitStack() as ctx:
+        held = ctx.enter_context(tc.tile_pool(name="held", bufs=1))
+        psum = ctx.enter_context(tc.psum_pool(name="psum", bufs=1))
+
+        offsets = held.tile([P, N // 16], U16, name="offsets")
+        k_raw = [held.tile([P, 2, T], F32, name=f"k_raw{u}") for u in range(2)]
+        k_pairs = [held.tile([P, 2 * T], BF16, name=f"k_pairs{u}", align_bytes=64) for u in range(2)]
+        v_parts = [(0, 640), (640, T)]
+        v_raw = [held.tile([P, 2, b - a], F32, name=f"v_raw{h}", tag=f"v_raw{h}") for h, (a, b) in enumerate(v_parts)]
+        v_pairs = held.tile([P, 2 * T], BF16, name="v_pairs", tag="v_pairs", align_bytes=64)
+        q_raw = held.tile([P, 4, NQ], F32, name="q_raw")
+        pos_pool = held.tile([P, T], F32, name="pos_pool")
+        vs_pool = held.tile([P, T], F32, name="vs_pool")
+        slope_col = held.tile([P, 1], F32, name="slope_col")
+
+        k_rows = kT.rearrange("(p t) n -> p t n", t=4)
+        v_rows = vT.rearrange("(p t) n -> p t n", t=2)
+
+        def load_half(tile, rows, h, parts=2):
+            cols = slice(h * (T // parts), (h + 1) * (T // parts))
+            nc.sync.dma_start(out=tile[:, :, cols], in_=rows[:, :, cols])
+
+        slope_rows = held.tile([P, P], F32, name="slope_rows")
+        nc.gpsimd.memset(slope_rows[:], 0.0)
+        load_half(k_raw[0], k_rows[:, 0:2, :], 0)
+        nc.sync.dma_start(offsets[:], offs)
+        nc.sync.dma_start(out=slope_rows[0:1, :], in_=slope[0].rearrange("q o -> o q"))
+        load_half(k_raw[0], k_rows[:, 0:2, :], 1)
+        load_half(k_raw[1], k_rows[:, 2:4, :], 0)
+        load_half(k_raw[1], k_rows[:, 2:4, :], 1)
+        nc.sync.dma_start(out=q_raw[:], in_=qT[0].rearrange("(p t) q -> p t q", t=4))
+        nc.sync.dma_start(out=pos_pool[:], in_=pos)
+        for h, (a, b) in enumerate(v_parts):
+            nc.sync.dma_start(out=v_raw[h][:], in_=v_rows[:, :, a:b])
+        nc.sync.dma_start(out=vs_pool[:], in_=vs)
+
+        warm = held.tile([P, 1], F32, name="warm")
+        warm_out = held.tile([P, 1], F32, name="warm_out")
+        nc.vector.memset(warm[:], 0.0)
+        nc.scalar.activation(warm_out[:], warm[:], EXP)
+        ident = held.tile([P, P], F32, name="ident")
+        make_identity(nc, ident[:])
+
+        def pair_up(engine, pairs, raw, a, b):
+            dst = pairs[:, 2 * a : 2 * b].rearrange("p (n t) -> p n t", t=2)
+            src = raw[:, :, a:b].rearrange("p t n -> p n t")
+            if engine == "scalar":
+                nc.scalar.activation(dst, src, COPY)
+            else:
+                nc.vector.tensor_copy(out=dst, in_=src)
+
+        def quantise(name, src, width):
+            codes = held.tile([P, width], U32, name=name + "_codes", align_bytes=64)
+            scales = held.tile([P, width], U8, name=name + "_scales", align_bytes=64)
+            return codes, scales
+
+        k_words = held.tile([P, N, 2], U32, name="k_words", align_bytes=64)
+        pair_up("scalar", k_pairs[0], k_raw[0], 0, 512)
+        pair_up("vector", k_pairs[0], k_raw[0], 512, 1024)
+        slope_bank = psum.tile([P, P], F32, name="slope_bank")
+        nc.tensor.transpose(slope_bank[:], slope_rows[:], ident[:])
+        nc.scalar.copy(slope_col[:], slope_bank[:, 0:1])
+        nc.vector.tensor_copy(k_words[:, :, 0], k_pairs[0][:].bitcast(U32).indirect(offsets[:]))
+        pair_up("scalar", k_pairs[1], k_raw[1], 0, 512)
+        pair_up("scalar", k_pairs[1], k_raw[1], 512, 624)
+        pair_up("vector", k_pairs[1], k_raw[1], 624, 1024)
+        nc.vector.tensor_copy(k_words[:, :, 1], k_pairs[1][:].bitcast(U32).indirect(offsets[:]))
+        q_grouped = held.tile([P, NQ, 4], BF16, name="q_grouped", align_bytes=64)
+        nc.scalar.activation(q_grouped[:], q_raw[:].rearrange("p t q -> p q t"), COPY)
+        q_codes, q_scales = quantise("q", None, NQ)
+        nc.vector.quantize_mx(out=q_codes[:].bitcast(FP8X4), scales=q_scales[:], in_=q_grouped[:].rearrange("p q t -> p (q t)"))
+        k_codes, k_scales = quantise("k", None, N)
+        k_flat = k_words[:].rearrange("p n u -> p (n u)").bitcast(BF16)
+        H = N // 2
+        scores = []
+        for h in range(2):
+            cols = slice(h * H, (h + 1) * H)
+            nc.vector.quantize_mx(out=k_codes[:, cols].bitcast(FP8X4), scales=k_scales[:, cols], in_=k_flat[:, 4 * h * H : 4 * (h + 1) * H])
+            bank = psum.tile([P, H], F32, name=f"scores{h}")
+            nc.tensor.matmul_mx(out=bank[:], lhsT=q_codes[:].bitcast(FP8X4), lhsT_scale=q_scales[:], rhs=k_codes[:, cols].bitcast(FP8X4), rhs_scale=k_scales[:, cols], start=True, stop=True)
+            scores.append(bank)
+
+        v_dst = [v_pairs[:, 2 * a : 2 * b].rearrange("p (n t) -> p n t", t=2) for a, b in v_parts]
+        nc.scalar.activation(v_dst[0], v_raw[0][:].rearrange("p t n -> p n t"), COPY)
+        pos_listed = held.tile([P, N], F32, name="pos_listed")
+        nc.vector.tensor_copy(pos_listed[:], pos_pool[:].indirect(offsets[:]))
+        s = held.tile([P, N], F32, name="s")
+        for h in range(2):
+            cols = slice(h * H, (h + 1) * H)
+            nc.vector.scalar_tensor_tensor(out=s[:, cols], in0=pos_listed[:, cols], scalar=slope_col[:], in1=scores[h][:], op0=MULT, op1=ADD)
+        nc.vector.tensor_copy(out=v_dst[1], in_=v_raw[1][:].rearrange("p t n -> p n t"))
+        minus_m = held.tile([P, 1], F32, name="minus_m", tag="v_raw1")
+        nc.vector.tensor_reduce(out=minus_m[:], in_=s[:], axis=X, op=MAX, negate=True)
+
+        s4 = s[:].rearrange("p (i u e) -> p i u e", u=2, e=2)
+        pr, sums = [], []
+        for u in range(2):
+            pu = held.tile([P, N // 4, 2], F32, name=f"p{u}", tag="v_raw0" if u == 0 else "p1")
+            su = held.tile([P, 1], F32, name=f"sum{u}")
+            nc.scalar.activation(pu[:], s4[:, :, u, :], EXP, bias=minus_m[:], accum_out=su[:])
+            pr.append(pu)
+            sums.append(su)
+
+        v_words = held.tile([P, 4, N // 4], U32, name="v_words", align_bytes=64)
+        nc.vector.tensor_copy(v_words[:].rearrange("p t i -> p i t"), v_pairs[:].bitcast(U32).indirect(offsets[:]))
+        v_bank = psum.tile([P, 4, P], F32, name="v_bank")
+        for t in range(4):
+            nc.tensor.transpose(v_bank[:, t, :], v_words[:, t, :].bitcast(F32), ident[:])
+        v_grouped = held.tile([P, DV, 4], BF16, name="v_grouped", align_bytes=64)
+        v_turned = v_bank[:].rearrange("p t w -> p (t w)").bitcast(BF16).rearrange("p (t e) -> p e t", t=4)
+        nc.scalar.copy(v_grouped[:, 0:P, :], v_turned[:, 0:P, :])
+        v_codes, v_scales = quantise("v", None, DV)
+
+        vs_listed = held.tile([P, N], F32, name="vs_listed", tag="v_pairs", align_bytes=64)
+        nc.vector.tensor_copy(vs_listed[:], vs_pool[:].indirect(offsets[:]))
+        vs4 = vs_listed[:].rearrange("p (i u e) -> p i u e", u=2, e=2)
+        w_bank = psum.tile([P, 2, P], F32, name="w_bank")
+        for u in range(2):
+            wu = held.tile([P, N // 4, 2], BF16, name=f"w{u}", align_bytes=64)
+            nc.vector.tensor_tensor(wu[:], pr[u][:], vs4[:, :, u, :], MULT)
+            nc.tensor.transpose(w_bank[:, u, :], wu[:].rearrange("p i e -> p (i e)").bitcast(F32), ident[:])
+        total = held.tile([P, 1], F32, name="total")
+        nc.vector.tensor_tensor(total[:], sums[0][:], sums[1][:], ADD)
+        inv = held.tile([P, 1], F32, name="inv")
+        nc.vector.reciprocal(inv[:], total[:])
+        nc.vector.tensor_copy(out=v_grouped[:, P:DV, :], in_=v_turned[:, P:DV, :])
+        nc.vector.quantize_mx(out=v_codes[:, 0:128].bitcast(FP8X4), scales=v_scales[:, 0:128], in_=v_grouped[:, 0:128, :].rearrange("p e t -> p (e t)"))
+        nc.vector.quantize_mx(out=v_codes[:, 128:256].bitcast(FP8X4), scales=v_scales[:, 128:256], in_=v_grouped[:, 128:256, :].rearrange("p e t -> p (e t)"))
+        w_grouped = held.tile([P, NQ, 4], BF16, name="w_grouped", align_bytes=64)
+        w_words = w_grouped[:].rearrange("p q t -> p (q t)").bitcast(F32).rearrange("p (q u) -> p q u", u=2)
+        nc.scalar.copy(w_words, w_bank[:].rearrange("p u q -> p q u"))
+        w_codes, w_scales = quantise("w", None, NQ)
+        nc.vector.quantize_mx(out=w_codes[:].bitcast(FP8X4), scales=w_scales[:], in_=w_grouped[:].rearrange("p q t -> p (q t)"))
+
+        HV = DV // 2
+        for h in range(2):
+            cols = slice(h * HV, (h + 1) * HV)
+            y = psum.tile([P, HV], F32, name=f"y{h}")
+            nc.tensor.matmul_mx(out=y[:], lhsT=w_codes[:].bitcast(FP8X4), lhsT_scale=w_scales[:], rhs=v_codes[:, cols].bitcast(FP8X4), rhs_scale=v_scales[:, cols], start=True, stop=True)
+            res = held.tile([P, HV], F32, name=f"res{h}")
+            if h == 0:
+                nc.scalar.activation(res[:], y[:], COPY, scale=inv[:])
+            else:
+                nc.vector.tensor_scalar(res[:], y[:], inv[:], None, MULT)
+            nc.sync.dma_start(out=out[0][:, cols], in_=res[:])

@@ -5,6 +5,7 @@ from concourse.masks import make_identity
 
 NQ, D, N, T, DV = 128, 512, 512, 1024, 256
 P = 128
+LAST = P - 1
 FLOPS = 2 * NQ * N * (D + DV)
 
 F32 = mybir.dt.float32
@@ -28,34 +29,30 @@ def tile_attend_ring_alibi_kernel(tc, qT, kT, vT, vs, pos, slope, offs, out):
         offsets = held.tile([P, N // 16], U16, name="offsets")
         k_raw = [held.tile([P, 2, T], F32, name=f"k_raw{u}") for u in range(2)]
         k_pairs = [held.tile([P, 2 * T], BF16, name=f"k_pairs{u}", align_bytes=64) for u in range(2)]
-        v_parts = [(0, 640), (640, T)]
-        v_raw = [held.tile([P, 2, b - a], F32, name=f"v_raw{h}", tag=f"v_raw{h}") for h, (a, b) in enumerate(v_parts)]
-        v_pairs = held.tile([P, 2 * T], BF16, name="v_pairs", tag="v_pairs", align_bytes=64)
+        v_raw = [held.tile([P, T], F32, name=f"v_raw{j}") for j in range(2)]
         q_raw = held.tile([P, 4, NQ], F32, name="q_raw")
         pos_pool = held.tile([P, T], F32, name="pos_pool")
         vs_pool = held.tile([P, T], F32, name="vs_pool")
         slope_col = held.tile([P, 1], F32, name="slope_col")
 
         k_rows = kT.rearrange("(p t) n -> p t n", t=4)
-        v_rows = vT.rearrange("(p t) n -> p t n", t=2)
 
-        def load_half(tile, rows, h, parts=2):
-            cols = slice(h * (T // parts), (h + 1) * (T // parts))
-            nc.sync.dma_start(out=tile[:, :, cols], in_=rows[:, :, cols])
+        def load_cols(tile, rows, a, b):
+            nc.sync.dma_start(out=tile[:, :, a:b], in_=rows[:, :, a:b])
 
-        slope_rows = held.tile([P, P], F32, name="slope_rows")
-        nc.gpsimd.memset(slope_rows[:], 0.0)
-        load_half(k_raw[0], k_rows[:, 0:2, :], 0)
+        nc.vector.memset(pos_pool[0:LAST, :], 0.0)
+        nc.vector.memset(vs_pool[0:LAST, :], 0.0)
         nc.sync.dma_start(offsets[:], offs)
-        nc.sync.dma_start(out=slope_rows[0:1, :], in_=slope[0].rearrange("q o -> o q"))
-        load_half(k_raw[0], k_rows[:, 0:2, :], 1)
-        load_half(k_raw[1], k_rows[:, 2:4, :], 0)
-        load_half(k_raw[1], k_rows[:, 2:4, :], 1)
+        load_cols(k_raw[0], k_rows[:, 0:2, :], 0, 512)
+        nc.scalar.dma_start(out=pos_pool[LAST:P, :], in_=pos[0:1, :])
+        nc.scalar.dma_start(out=vs_pool[LAST:P, :], in_=vs[0:1, :])
+        load_cols(k_raw[0], k_rows[:, 0:2, :], 512, T)
+        load_cols(k_raw[1], k_rows[:, 2:4, :], 0, 512)
+        load_cols(k_raw[1], k_rows[:, 2:4, :], 512, T)
+        nc.sync.dma_start(out=slope_col[:], in_=slope[0])
         nc.sync.dma_start(out=q_raw[:], in_=qT[0].rearrange("(p t) q -> p t q", t=4))
-        nc.sync.dma_start(out=pos_pool[:], in_=pos)
-        for h, (a, b) in enumerate(v_parts):
-            nc.sync.dma_start(out=v_raw[h][:], in_=v_rows[:, :, a:b])
-        nc.sync.dma_start(out=vs_pool[:], in_=vs)
+        for j in range(2):
+            nc.sync.dma_start(out=v_raw[j][:], in_=vT[j * P : (j + 1) * P, :])
 
         warm = held.tile([P, 1], F32, name="warm")
         warm_out = held.tile([P, 1], F32, name="warm_out")
@@ -72,93 +69,102 @@ def tile_attend_ring_alibi_kernel(tc, qT, kT, vT, vs, pos, slope, offs, out):
             else:
                 nc.vector.tensor_copy(out=dst, in_=src)
 
-        def quantise(name, src, width):
+        def planes(name, width):
             codes = held.tile([P, width], U32, name=name + "_codes", align_bytes=64)
             scales = held.tile([P, width], U8, name=name + "_scales", align_bytes=64)
             return codes, scales
 
-        k_words = held.tile([P, N, 2], U32, name="k_words", align_bytes=64)
+        pos_listed = held.tile([P, N], F32, name="pos_listed")
+        vs_listed = held.tile([P, N], F32, name="vs_listed")
+        nc.vector.tensor_copy(pos_listed[:], pos_pool[:].indirect(offsets[:]))
+        nc.vector.tensor_copy(vs_listed[:], vs_pool[:].indirect(offsets[:]))
         pair_up("scalar", k_pairs[0], k_raw[0], 0, 512)
-        pair_up("vector", k_pairs[0], k_raw[0], 512, 1024)
-        slope_bank = psum.tile([P, P], F32, name="slope_bank")
-        nc.tensor.transpose(slope_bank[:], slope_rows[:], ident[:])
-        nc.scalar.copy(slope_col[:], slope_bank[:, 0:1])
+        pos_bank = psum.tile([P, 4, P], F32, name="pos_bank", tag="p0")
+        for j in range(4):
+            nc.tensor.transpose(pos_bank[:, j, :], pos_listed[:, j * P : (j + 1) * P], ident[:])
+        pos_cols = held.tile([P, 4], F32, name="pos_cols")
+        nc.scalar.copy(pos_cols[:], pos_bank[:, :, LAST])
+        spread = psum.tile([P, N], F32, name="spread", tag="y0")
+        for j in range(4):
+            nc.tensor.transpose(spread[:, j * P : (j + 1) * P], pos_cols[:, j : j + 1].to_broadcast([P, P]), ident[:])
+        vs_bank = psum.tile([P, 4, P], F32, name="vs_bank", tag="p1")
+        for t in range(4):
+            nc.tensor.transpose(vs_bank[:, t, :], vs_listed[:, t : N : 4], ident[:])
+
+        k_words = held.tile([P, N, 2], U32, name="k_words", align_bytes=64)
+        pair_up("vector", k_pairs[0], k_raw[0], 512, T)
         nc.vector.tensor_copy(k_words[:, :, 0], k_pairs[0][:].bitcast(U32).indirect(offsets[:]))
         pair_up("scalar", k_pairs[1], k_raw[1], 0, 512)
         pair_up("scalar", k_pairs[1], k_raw[1], 512, 624)
-        pair_up("vector", k_pairs[1], k_raw[1], 624, 1024)
+        pair_up("vector", k_pairs[1], k_raw[1], 624, T)
         nc.vector.tensor_copy(k_words[:, :, 1], k_pairs[1][:].bitcast(U32).indirect(offsets[:]))
+        bias = held.tile([P, 4, P], F32, name="bias")
+        nc.scalar.activation(bias[:], spread[:].rearrange("p (i t) -> p t i", t=4), COPY, scale=slope_col[:])
         q_grouped = held.tile([P, NQ, 4], BF16, name="q_grouped", align_bytes=64)
         nc.scalar.activation(q_grouped[:], q_raw[:].rearrange("p t q -> p q t"), COPY)
-        q_codes, q_scales = quantise("q", None, NQ)
+        vs_cols = held.tile([P, 4], F32, name="vs_cols")
+        nc.scalar.copy(vs_cols[:], vs_bank[:, :, LAST])
+        q_codes, q_scales = planes("q", NQ)
         nc.vector.quantize_mx(out=q_codes[:].bitcast(FP8X4), scales=q_scales[:], in_=q_grouped[:].rearrange("p q t -> p (q t)"))
-        k_codes, k_scales = quantise("k", None, N)
+        k_codes, k_scales = planes("k", N)
         k_flat = k_words[:].rearrange("p n u -> p (n u)").bitcast(BF16)
         H = N // 2
         scores = []
         for h in range(2):
             cols = slice(h * H, (h + 1) * H)
             nc.vector.quantize_mx(out=k_codes[:, cols].bitcast(FP8X4), scales=k_scales[:, cols], in_=k_flat[:, 4 * h * H : 4 * (h + 1) * H])
-            bank = psum.tile([P, H], F32, name=f"scores{h}")
+            bank = psum.tile([P, H], F32, name=f"scores{h}", tag=f"scores{h}")
             nc.tensor.matmul_mx(out=bank[:], lhsT=q_codes[:].bitcast(FP8X4), lhsT_scale=q_scales[:], rhs=k_codes[:, cols].bitcast(FP8X4), rhs_scale=k_scales[:, cols], start=True, stop=True)
             scores.append(bank)
 
-        v_dst = [v_pairs[:, 2 * a : 2 * b].rearrange("p (n t) -> p n t", t=2) for a, b in v_parts]
-        nc.scalar.activation(v_dst[0], v_raw[0][:].rearrange("p t n -> p n t"), COPY)
-        pos_listed = held.tile([P, N], F32, name="pos_listed")
-        nc.vector.tensor_copy(pos_listed[:], pos_pool[:].indirect(offsets[:]))
-        s = held.tile([P, N], F32, name="s")
+        s = held.tile([P, 4, P], F32, name="s")
         for h in range(2):
-            cols = slice(h * H, (h + 1) * H)
-            nc.vector.scalar_tensor_tensor(out=s[:, cols], in0=pos_listed[:, cols], scalar=slope_col[:], in1=scores[h][:], op0=MULT, op1=ADD)
-        nc.vector.tensor_copy(out=v_dst[1], in_=v_raw[1][:].rearrange("p t n -> p n t"))
-        minus_m = held.tile([P, 1], F32, name="minus_m", tag="v_raw1")
-        nc.vector.tensor_reduce(out=minus_m[:], in_=s[:], axis=X, op=MAX, negate=True)
+            part = slice(h * 64, (h + 1) * 64)
+            nc.vector.tensor_tensor(s[:, :, part], scores[h][:].rearrange("p (i t) -> p t i", t=4), bias[:, :, part], ADD)
+        minus_m = held.tile([P, 1], F32, name="minus_m")
+        nc.vector.tensor_reduce(out=minus_m[:], in_=s[:].rearrange("p t i -> p (t i)"), axis=X, op=MAX, negate=True)
 
-        s4 = s[:].rearrange("p (i u e) -> p i u e", u=2, e=2)
-        pr, sums = [], []
+        p_banks, sums = [], []
         for u in range(2):
-            pu = held.tile([P, N // 4, 2], F32, name=f"p{u}", tag="v_raw0" if u == 0 else "p1")
+            pu = held.tile([P, 2, P], F32, name=f"p{u}")
             su = held.tile([P, 1], F32, name=f"sum{u}")
-            nc.scalar.activation(pu[:], s4[:, :, u, :], EXP, bias=minus_m[:], accum_out=su[:])
-            pr.append(pu)
+            nc.scalar.activation(pu[:], s[:, 2 * u : 2 * u + 2, :], EXP, bias=minus_m[:], accum_out=su[:])
+            bank = psum.tile([P, 2, P], F32, name=f"p_bank{u}", tag=f"p{u}")
+            for e in range(2):
+                nc.tensor.transpose(bank[:, e, :], pu[:, e, :], ident[:])
+            p_banks.append(bank)
             sums.append(su)
 
-        v_words = held.tile([P, 4, N // 4], U32, name="v_words", align_bytes=64)
-        nc.vector.tensor_copy(v_words[:].rearrange("p t i -> p i t"), v_pairs[:].bitcast(U32).indirect(offsets[:]))
-        v_bank = psum.tile([P, 4, P], F32, name="v_bank")
-        for t in range(4):
-            nc.tensor.transpose(v_bank[:, t, :], v_words[:, t, :].bitcast(F32), ident[:])
-        v_grouped = held.tile([P, DV, 4], BF16, name="v_grouped", align_bytes=64)
-        v_turned = v_bank[:].rearrange("p t w -> p (t w)").bitcast(BF16).rearrange("p (t e) -> p e t", t=4)
-        nc.scalar.copy(v_grouped[:, 0:P, :], v_turned[:, 0:P, :])
-        v_codes, v_scales = quantise("v", None, DV)
+        v_codes, v_scales = planes("v", DV)
+        v_grouped = []
+        for j in range(2):
+            listed = held.tile([P, 2, P, 2], BF16, name=f"v_listed{j}", align_bytes=64)
+            nc.vector.tensor_copy(listed[:].rearrange("p u s e -> p s u e"), v_raw[j][:].indirect(offsets[:]))
+            bank = psum.tile([P, 2, P], F32, name=f"v_bank{j}")
+            for u in range(2):
+                nc.tensor.transpose(bank[:, u, :], listed[:, u, :, :].rearrange("p s e -> p (s e)").bitcast(F32), ident[:])
+            grouped = held.tile([P, P, 4], BF16, name=f"v_grouped{j}", align_bytes=64)
+            words = grouped[:].rearrange("p e t -> p (e t)").bitcast(F32).rearrange("p (e u) -> p e u", u=2)
+            nc.scalar.copy(words, bank[:].rearrange("p u e -> p e u"))
+            v_grouped.append(grouped)
 
-        vs_listed = held.tile([P, N], F32, name="vs_listed", tag="v_pairs", align_bytes=64)
-        nc.vector.tensor_copy(vs_listed[:], vs_pool[:].indirect(offsets[:]))
-        vs4 = vs_listed[:].rearrange("p (i u e) -> p i u e", u=2, e=2)
-        w_bank = psum.tile([P, 2, P], F32, name="w_bank")
+        w_grouped = held.tile([P, NQ, 4], BF16, name="w_grouped", align_bytes=64)
         for u in range(2):
-            wu = held.tile([P, N // 4, 2], BF16, name=f"w{u}", align_bytes=64)
-            nc.vector.tensor_tensor(wu[:], pr[u][:], vs4[:, :, u, :], MULT)
-            nc.tensor.transpose(w_bank[:, u, :], wu[:].rearrange("p i e -> p (i e)").bitcast(F32), ident[:])
+            pair = slice(2 * u, 2 * u + 2)
+            nc.vector.tensor_tensor(w_grouped[:, :, pair], p_banks[u][:].rearrange("p e q -> p q e"), vs_cols[:, pair].unsqueeze(1).to_broadcast([P, NQ, 2]), MULT)
+        nc.vector.quantize_mx(out=v_codes[:, 0:128].bitcast(FP8X4), scales=v_scales[:, 0:128], in_=v_grouped[0][:].rearrange("p e t -> p (e t)"))
+        w_codes, w_scales = planes("w", NQ)
+        nc.vector.quantize_mx(out=w_codes[:].bitcast(FP8X4), scales=w_scales[:], in_=w_grouped[:].rearrange("p q t -> p (q t)"))
+        nc.vector.quantize_mx(out=v_codes[:, 128:256].bitcast(FP8X4), scales=v_scales[:, 128:256], in_=v_grouped[1][:].rearrange("p e t -> p (e t)"))
         total = held.tile([P, 1], F32, name="total")
         nc.vector.tensor_tensor(total[:], sums[0][:], sums[1][:], ADD)
         inv = held.tile([P, 1], F32, name="inv")
         nc.vector.reciprocal(inv[:], total[:])
-        nc.vector.tensor_copy(out=v_grouped[:, P:DV, :], in_=v_turned[:, P:DV, :])
-        nc.vector.quantize_mx(out=v_codes[:, 0:128].bitcast(FP8X4), scales=v_scales[:, 0:128], in_=v_grouped[:, 0:128, :].rearrange("p e t -> p (e t)"))
-        nc.vector.quantize_mx(out=v_codes[:, 128:256].bitcast(FP8X4), scales=v_scales[:, 128:256], in_=v_grouped[:, 128:256, :].rearrange("p e t -> p (e t)"))
-        w_grouped = held.tile([P, NQ, 4], BF16, name="w_grouped", align_bytes=64)
-        w_words = w_grouped[:].rearrange("p q t -> p (q t)").bitcast(F32).rearrange("p (q u) -> p q u", u=2)
-        nc.scalar.copy(w_words, w_bank[:].rearrange("p u q -> p q u"))
-        w_codes, w_scales = quantise("w", None, NQ)
-        nc.vector.quantize_mx(out=w_codes[:].bitcast(FP8X4), scales=w_scales[:], in_=w_grouped[:].rearrange("p q t -> p (q t)"))
 
         HV = DV // 2
         for h in range(2):
             cols = slice(h * HV, (h + 1) * HV)
-            y = psum.tile([P, HV], F32, name=f"y{h}")
+            y = psum.tile([P, HV], F32, name=f"y{h}", tag="y0" if h == 0 else "scores0")
             nc.tensor.matmul_mx(out=y[:], lhsT=w_codes[:].bitcast(FP8X4), lhsT_scale=w_scales[:], rhs=v_codes[:, cols].bitcast(FP8X4), rhs_scale=v_scales[:, cols], start=True, stop=True)
             res = held.tile([P, HV], F32, name=f"res{h}")
             if h == 0:

@@ -17,6 +17,7 @@ FP8X4 = mybir.dt.float8_e4m3fn_x4
 ADD, MULT, MAX = mybir.AluOpType.add, mybir.AluOpType.mult, mybir.AluOpType.max
 EXP = mybir.ActivationFunctionType.Exp
 COPY = mybir.ActivationFunctionType.Copy
+IDENTITY = mybir.ActivationFunctionType.Identity
 X = mybir.AxisListType.X
 
 
@@ -29,11 +30,11 @@ def tile_attend_ring_alibi_kernel(tc, qT, kT, vT, vs, pos, slope, offs, out):
         offsets = held.tile([P, N // 16], U16, name="offsets")
         k_raw = [held.tile([P, 2, T], F32, name=f"k_raw{u}") for u in range(2)]
         k_pairs = [held.tile([P, 2 * T], BF16, name=f"k_pairs{u}", align_bytes=64) for u in range(2)]
-        v_raw = [held.tile([P, T], F32, name=f"v_raw{j}") for j in range(2)]
-        q_raw = held.tile([P, 4, NQ], F32, name="q_raw")
+        v_raw = [held.tile([P, T], F32, name=f"v_raw{j}", tag=f"v_raw{j}", align_bytes=64) for j in range(2)]
+        q_raw = held.tile([P, 4, NQ], F32, name="q_raw", tag="v_round", align_bytes=64)
         pos_pool = held.tile([P, T], F32, name="pos_pool")
         vs_pool = held.tile([P, T], F32, name="vs_pool")
-        slope_col = held.tile([P, 1], F32, name="slope_col")
+        slope_col = held.tile([P, 1], F32, name="slope_col", tag="v_listed0", align_bytes=64)
 
         k_rows = kT.rearrange("(p t) n -> p t n", t=4)
 
@@ -46,13 +47,14 @@ def tile_attend_ring_alibi_kernel(tc, qT, kT, vT, vs, pos, slope, offs, out):
         load_cols(k_raw[0], k_rows[:, 0:2, :], 0, 512)
         nc.scalar.dma_start(out=pos_pool[LAST:P, :], in_=pos[0:1, :])
         nc.scalar.dma_start(out=vs_pool[LAST:P, :], in_=vs[0:1, :])
+        nc.sync.dma_start(out=slope_col[:], in_=slope[0])
         load_cols(k_raw[0], k_rows[:, 0:2, :], 512, T)
         load_cols(k_raw[1], k_rows[:, 2:4, :], 0, 512)
         load_cols(k_raw[1], k_rows[:, 2:4, :], 512, T)
-        nc.sync.dma_start(out=slope_col[:], in_=slope[0])
         nc.sync.dma_start(out=q_raw[:], in_=qT[0].rearrange("(p t) q -> p t q", t=4))
-        for j in range(2):
-            nc.sync.dma_start(out=v_raw[j][:], in_=vT[j * P : (j + 1) * P, :])
+        for h in range(2):
+            nc.sync.dma_start(out=v_raw[0][:, h * 512 : (h + 1) * 512], in_=vT[0:P, h * 512 : (h + 1) * 512])
+        nc.sync.dma_start(out=v_raw[1][:], in_=vT[P : 2 * P, :])
 
         warm = held.tile([P, 1], F32, name="warm")
         warm_out = held.tile([P, 1], F32, name="warm_out")
@@ -70,7 +72,7 @@ def tile_attend_ring_alibi_kernel(tc, qT, kT, vT, vs, pos, slope, offs, out):
                 nc.vector.tensor_copy(out=dst, in_=src)
 
         def planes(name, width):
-            codes = held.tile([P, width], U32, name=name + "_codes", align_bytes=64)
+            codes = held.tile([P, width], U32, name=name + "_codes", tag=name + "_codes", align_bytes=64)
             scales = held.tile([P, width], U8, name=name + "_scales", align_bytes=64)
             return codes, scales
 
@@ -98,11 +100,11 @@ def tile_attend_ring_alibi_kernel(tc, qT, kT, vT, vs, pos, slope, offs, out):
         pair_up("scalar", k_pairs[1], k_raw[1], 512, 624)
         pair_up("vector", k_pairs[1], k_raw[1], 624, T)
         nc.vector.tensor_copy(k_words[:, :, 1], k_pairs[1][:].bitcast(U32).indirect(offsets[:]))
-        bias = held.tile([P, 4, P], F32, name="bias")
+        bias = held.tile([P, 4, P], F32, name="bias", tag="bias", align_bytes=64)
         nc.scalar.activation(bias[:], spread[:].rearrange("p (i t) -> p t i", t=4), COPY, scale=slope_col[:])
         q_grouped = held.tile([P, NQ, 4], BF16, name="q_grouped", align_bytes=64)
         nc.scalar.activation(q_grouped[:], q_raw[:].rearrange("p t q -> p q t"), COPY)
-        vs_cols = held.tile([P, 4], F32, name="vs_cols")
+        vs_cols = held.tile([P, 4], F32, name="vs_cols", tag="v_codes", align_bytes=64)
         nc.scalar.copy(vs_cols[:], vs_bank[:, :, LAST])
         q_codes, q_scales = planes("q", NQ)
         nc.vector.quantize_mx(out=q_codes[:].bitcast(FP8X4), scales=q_scales[:], in_=q_grouped[:].rearrange("p q t -> p (q t)"))
@@ -117,6 +119,12 @@ def tile_attend_ring_alibi_kernel(tc, qT, kT, vT, vs, pos, slope, offs, out):
             nc.tensor.matmul_mx(out=bank[:], lhsT=q_codes[:].bitcast(FP8X4), lhsT_scale=q_scales[:], rhs=k_codes[:, cols].bitcast(FP8X4), rhs_scale=k_scales[:, cols], start=True, stop=True)
             scores.append(bank)
 
+        v_round = held.tile([P, T], BF16, name="v_round", tag="v_round", align_bytes=64)
+        for h in range(2):
+            nc.scalar.activation(v_round[:, h * 512 : (h + 1) * 512], v_raw[0][:, h * 512 : (h + 1) * 512], COPY)
+        v_listed0 = held.tile([P, 2, P, 2], BF16, name="v_listed0", tag="v_listed0", align_bytes=64)
+        nc.scalar.activation(v_listed0[:].rearrange("p u s e -> p s u e"), v_round[:].indirect(offsets[:]), COPY)
+
         s = held.tile([P, 4, P], F32, name="s")
         for h in range(2):
             part = slice(h * 64, (h + 1) * 64)
@@ -126,7 +134,7 @@ def tile_attend_ring_alibi_kernel(tc, qT, kT, vT, vs, pos, slope, offs, out):
 
         p_banks, sums = [], []
         for u in range(2):
-            pu = held.tile([P, 2, P], F32, name=f"p{u}")
+            pu = held.tile([P, 2, P], F32, name=f"p{u}", tag="v_round" if u == 0 else "p1", align_bytes=64)
             su = held.tile([P, 1], F32, name=f"sum{u}")
             nc.scalar.activation(pu[:], s[:, 2 * u : 2 * u + 2, :], EXP, bias=minus_m[:], accum_out=su[:])
             bank = psum.tile([P, 2, P], F32, name=f"p_bank{u}", tag=f"p{u}")
@@ -136,28 +144,31 @@ def tile_attend_ring_alibi_kernel(tc, qT, kT, vT, vs, pos, slope, offs, out):
             sums.append(su)
 
         v_codes, v_scales = planes("v", DV)
-        v_grouped = []
-        for j in range(2):
-            listed = held.tile([P, 2, P, 2], BF16, name=f"v_listed{j}", align_bytes=64)
-            nc.vector.tensor_copy(listed[:].rearrange("p u s e -> p s u e"), v_raw[j][:].indirect(offsets[:]))
-            bank = psum.tile([P, 2, P], F32, name=f"v_bank{j}")
+
+        def turn_values(j, halves, tag):
+            bank = psum.tile([P, 2, P], F32, name=f"v_bank{j}", tag=tag)
             for u in range(2):
-                nc.tensor.transpose(bank[:, u, :], listed[:, u, :, :].rearrange("p s e -> p (s e)").bitcast(F32), ident[:])
+                nc.tensor.transpose(bank[:, u, :], halves[u], ident[:])
             grouped = held.tile([P, P, 4], BF16, name=f"v_grouped{j}", align_bytes=64)
             words = grouped[:].rearrange("p e t -> p (e t)").bitcast(F32).rearrange("p (e u) -> p e u", u=2)
             nc.scalar.copy(words, bank[:].rearrange("p u e -> p e u"))
-            v_grouped.append(grouped)
+            return grouped
 
-        w_grouped = held.tile([P, NQ, 4], BF16, name="w_grouped", align_bytes=64)
+        v_grouped0 = turn_values(0, [v_listed0[:, u, :, :].rearrange("p s e -> p (s e)").bitcast(F32) for u in range(2)], "v_bank0")
+        v_listed1 = held.tile([P, N], BF16, name="v_listed1", tag="bias", align_bytes=64)
+        nc.vector.tensor_copy(v_listed1[:], v_raw[1][:].indirect(offsets[:]))
+
+        w_grouped = held.tile([P, NQ, 4], BF16, name="w_grouped", tag="v_raw1", align_bytes=64)
         for u in range(2):
             pair = slice(2 * u, 2 * u + 2)
             nc.vector.tensor_tensor(w_grouped[:, :, pair], p_banks[u][:].rearrange("p e q -> p q e"), vs_cols[:, pair].unsqueeze(1).to_broadcast([P, NQ, 2]), MULT)
-        nc.vector.quantize_mx(out=v_codes[:, 0:128].bitcast(FP8X4), scales=v_scales[:, 0:128], in_=v_grouped[0][:].rearrange("p e t -> p (e t)"))
+        v_grouped1 = turn_values(1, [v_listed1[:].bitcast(F32)[:, u : N // 2 : 2] for u in range(2)], "p0")
+        nc.vector.quantize_mx(out=v_codes[:, 0:128].bitcast(FP8X4), scales=v_scales[:, 0:128], in_=v_grouped0[:].rearrange("p e t -> p (e t)"))
         w_codes, w_scales = planes("w", NQ)
         nc.vector.quantize_mx(out=w_codes[:].bitcast(FP8X4), scales=w_scales[:], in_=w_grouped[:].rearrange("p q t -> p (q t)"))
-        nc.vector.quantize_mx(out=v_codes[:, 128:256].bitcast(FP8X4), scales=v_scales[:, 128:256], in_=v_grouped[1][:].rearrange("p e t -> p (e t)"))
+        nc.vector.quantize_mx(out=v_codes[:, 128:256].bitcast(FP8X4), scales=v_scales[:, 128:256], in_=v_grouped1[:].rearrange("p e t -> p (e t)"))
         total = held.tile([P, 1], F32, name="total")
-        nc.vector.tensor_tensor(total[:], sums[0][:], sums[1][:], ADD)
+        nc.scalar.activation(total[:], sums[0][:], IDENTITY, bias=sums[1][:])
         inv = held.tile([P, 1], F32, name="inv")
         nc.vector.reciprocal(inv[:], total[:])
 

@@ -28,13 +28,12 @@ def tile_attend_ring_alibi_kernel(tc, qT, kT, vT, vs, pos, slope, offs, out):
         psum = ctx.enter_context(tc.psum_pool(name="psum", bufs=1))
 
         offsets = held.tile([P, N // 16], U16, name="offsets")
-        k_raw = [held.tile([P, 2, T], F32, name=f"k_raw{u}") for u in range(2)]
-        k_pairs = [held.tile([P, 2 * T], BF16, name=f"k_pairs{u}", align_bytes=64) for u in range(2)]
+        k_raw = [held.tile([P, 2, T], F32, name=f"k_raw{u}", tag=f"k_raw{u}", align_bytes=64) for u in range(2)]
         v_raw = [held.tile([P, T], F32, name=f"v_raw{j}", tag=f"v_raw{j}", align_bytes=64) for j in range(2)]
         q_raw = held.tile([P, 4, NQ], F32, name="q_raw", tag="v_round", align_bytes=64)
         pos_pool = held.tile([P, T], F32, name="pos_pool")
         vs_pool = held.tile([P, T], F32, name="vs_pool")
-        slope_col = held.tile([P, 1], F32, name="slope_col", tag="v_listed0", align_bytes=64)
+        slope_col = held.tile([P, 1], F32, name="slope_col", tag="k_codes", align_bytes=64)
 
         k_rows = kT.rearrange("(p t) n -> p t n", t=4)
 
@@ -47,10 +46,11 @@ def tile_attend_ring_alibi_kernel(tc, qT, kT, vT, vs, pos, slope, offs, out):
         load_cols(k_raw[0], k_rows[:, 0:2, :], 0, 512)
         nc.scalar.dma_start(out=pos_pool[LAST:P, :], in_=pos[0:1, :])
         nc.scalar.dma_start(out=vs_pool[LAST:P, :], in_=vs[0:1, :])
-        nc.sync.dma_start(out=slope_col[:], in_=slope[0])
+        nc.scalar.dma_start(out=slope_col[:], in_=slope[0])
         load_cols(k_raw[0], k_rows[:, 0:2, :], 512, T)
         load_cols(k_raw[1], k_rows[:, 2:4, :], 0, 512)
-        load_cols(k_raw[1], k_rows[:, 2:4, :], 512, T)
+        load_cols(k_raw[1], k_rows[:, 2:4, :], 512, 768)
+        load_cols(k_raw[1], k_rows[:, 2:4, :], 768, T)
         nc.sync.dma_start(out=q_raw[:], in_=qT[0].rearrange("(p t) q -> p t q", t=4))
         for h in range(2):
             nc.sync.dma_start(out=v_raw[0][:, h * 512 : (h + 1) * 512], in_=vT[0:P, h * 512 : (h + 1) * 512])
@@ -71,12 +71,13 @@ def tile_attend_ring_alibi_kernel(tc, qT, kT, vT, vs, pos, slope, offs, out):
             else:
                 nc.vector.tensor_copy(out=dst, in_=src)
 
-        def planes(name, width):
-            codes = held.tile([P, width], U32, name=name + "_codes", tag=name + "_codes", align_bytes=64)
+        def planes(name, width, tag):
+            codes = held.tile([P, width], U32, name=name + "_codes", tag=tag, align_bytes=64)
             scales = held.tile([P, width], U8, name=name + "_scales", align_bytes=64)
             return codes, scales
 
-        pos_listed = held.tile([P, N], F32, name="pos_listed")
+        pos_listed = held.tile([P, N], F32, name="pos_listed", tag="k_pairs1", align_bytes=64)
+        k_pairs = [held.tile([P, 2 * T], BF16, name="k_pairs0", align_bytes=64)]
         vs_listed = held.tile([P, N], F32, name="vs_listed")
         nc.vector.tensor_copy(pos_listed[:], pos_pool[:].indirect(offsets[:]))
         nc.vector.tensor_copy(vs_listed[:], vs_pool[:].indirect(offsets[:]))
@@ -89,26 +90,29 @@ def tile_attend_ring_alibi_kernel(tc, qT, kT, vT, vs, pos, slope, offs, out):
         spread = psum.tile([P, N], F32, name="spread", tag="y0")
         for j in range(4):
             nc.tensor.transpose(spread[:, j * P : (j + 1) * P], pos_cols[:, j : j + 1].to_broadcast([P, P]), ident[:])
-        vs_bank = psum.tile([P, 4, P], F32, name="vs_bank", tag="p1")
+        vs_bank = psum.tile([P, 4, P], F32, name="vs_bank", tag="p0")
         for t in range(4):
             nc.tensor.transpose(vs_bank[:, t, :], vs_listed[:, t : N : 4], ident[:])
 
         k_words = held.tile([P, N, 2], U32, name="k_words", align_bytes=64)
         pair_up("vector", k_pairs[0], k_raw[0], 512, T)
         nc.vector.tensor_copy(k_words[:, :, 0], k_pairs[0][:].bitcast(U32).indirect(offsets[:]))
+        k_pairs.append(held.tile([P, 2 * T], BF16, name="k_pairs1", tag="k_pairs1", align_bytes=64))
         pair_up("scalar", k_pairs[1], k_raw[1], 0, 512)
-        pair_up("scalar", k_pairs[1], k_raw[1], 512, 624)
-        pair_up("vector", k_pairs[1], k_raw[1], 624, T)
-        nc.vector.tensor_copy(k_words[:, :, 1], k_pairs[1][:].bitcast(U32).indirect(offsets[:]))
-        bias = held.tile([P, 4, P], F32, name="bias", tag="bias", align_bytes=64)
+        pair_up("vector", k_pairs[1], k_raw[1], 512, 768)
+        pair_up("scalar", k_pairs[1], k_raw[1], 768, 832)
+        pair_up("vector", k_pairs[1], k_raw[1], 832, T)
+        for h in range(2):
+            nc.vector.tensor_copy(k_words[:, h * 256 : (h + 1) * 256, 1], k_pairs[1][:].bitcast(U32).indirect(offsets[:, h * 16 : (h + 1) * 16]))
+        bias = held.tile([P, 4, P], F32, name="bias", tag="k_raw1", align_bytes=64)
         nc.scalar.activation(bias[:], spread[:].rearrange("p (i t) -> p t i", t=4), COPY, scale=slope_col[:])
-        q_grouped = held.tile([P, NQ, 4], BF16, name="q_grouped", align_bytes=64)
+        q_grouped = held.tile([P, NQ, 4], BF16, name="q_grouped", tag="k_codes", align_bytes=64)
         nc.scalar.activation(q_grouped[:], q_raw[:].rearrange("p t q -> p q t"), COPY)
-        vs_cols = held.tile([P, 4], F32, name="vs_cols", tag="v_codes", align_bytes=64)
-        nc.scalar.copy(vs_cols[:], vs_bank[:, :, LAST])
-        q_codes, q_scales = planes("q", NQ)
+        vs_cols = held.tile([P, 4], F32, name="vs_cols", tag="k_pairs1", align_bytes=64)
+        nc.vector.tensor_copy(vs_cols[:], vs_bank[:, :, LAST])
+        q_codes, q_scales = planes("q", NQ, "q_codes")
         nc.vector.quantize_mx(out=q_codes[:].bitcast(FP8X4), scales=q_scales[:], in_=q_grouped[:].rearrange("p q t -> p (q t)"))
-        k_codes, k_scales = planes("k", N)
+        k_codes, k_scales = planes("k", N, "k_codes")
         k_flat = k_words[:].rearrange("p n u -> p (n u)").bitcast(BF16)
         H = N // 2
         scores = []
@@ -125,7 +129,7 @@ def tile_attend_ring_alibi_kernel(tc, qT, kT, vT, vs, pos, slope, offs, out):
         v_listed0 = held.tile([P, 2, P, 2], BF16, name="v_listed0", tag="v_listed0", align_bytes=64)
         nc.scalar.activation(v_listed0[:].rearrange("p u s e -> p s u e"), v_round[:].indirect(offsets[:]), COPY)
 
-        s = held.tile([P, 4, P], F32, name="s")
+        s = held.tile([P, 4, P], F32, name="s", tag="s", align_bytes=64)
         for h in range(2):
             part = slice(h * 64, (h + 1) * 64)
             nc.vector.tensor_tensor(s[:, :, part], scores[h][:].rearrange("p (i t) -> p t i", t=4), bias[:, :, part], ADD)
@@ -143,19 +147,19 @@ def tile_attend_ring_alibi_kernel(tc, qT, kT, vT, vs, pos, slope, offs, out):
             p_banks.append(bank)
             sums.append(su)
 
-        v_codes, v_scales = planes("v", DV)
+        v_codes, v_scales = planes("v", DV, "k_pairs1")
 
         def turn_values(j, halves, tag):
             bank = psum.tile([P, 2, P], F32, name=f"v_bank{j}", tag=tag)
             for u in range(2):
                 nc.tensor.transpose(bank[:, u, :], halves[u], ident[:])
-            grouped = held.tile([P, P, 4], BF16, name=f"v_grouped{j}", align_bytes=64)
+            grouped = held.tile([P, P, 4], BF16, name=f"v_grouped{j}", tag="s" if j == 0 else "v_grouped1", align_bytes=64)
             words = grouped[:].rearrange("p e t -> p (e t)").bitcast(F32).rearrange("p (e u) -> p e u", u=2)
             nc.scalar.copy(words, bank[:].rearrange("p u e -> p e u"))
             return grouped
 
         v_grouped0 = turn_values(0, [v_listed0[:, u, :, :].rearrange("p s e -> p (s e)").bitcast(F32) for u in range(2)], "v_bank0")
-        v_listed1 = held.tile([P, N], BF16, name="v_listed1", tag="bias", align_bytes=64)
+        v_listed1 = held.tile([P, N], BF16, name="v_listed1", tag="k_raw1", align_bytes=64)
         nc.vector.tensor_copy(v_listed1[:], v_raw[1][:].indirect(offsets[:]))
 
         w_grouped = held.tile([P, NQ, 4], BF16, name="w_grouped", tag="v_raw1", align_bytes=64)
@@ -164,12 +168,12 @@ def tile_attend_ring_alibi_kernel(tc, qT, kT, vT, vs, pos, slope, offs, out):
             nc.vector.tensor_tensor(w_grouped[:, :, pair], p_banks[u][:].rearrange("p e q -> p q e"), vs_cols[:, pair].unsqueeze(1).to_broadcast([P, NQ, 2]), MULT)
         v_grouped1 = turn_values(1, [v_listed1[:].bitcast(F32)[:, u : N // 2 : 2] for u in range(2)], "p0")
         nc.vector.quantize_mx(out=v_codes[:, 0:128].bitcast(FP8X4), scales=v_scales[:, 0:128], in_=v_grouped0[:].rearrange("p e t -> p (e t)"))
-        w_codes, w_scales = planes("w", NQ)
+        w_codes, w_scales = planes("w", NQ, "w_codes")
         nc.vector.quantize_mx(out=w_codes[:].bitcast(FP8X4), scales=w_scales[:], in_=w_grouped[:].rearrange("p q t -> p (q t)"))
         nc.vector.quantize_mx(out=v_codes[:, 128:256].bitcast(FP8X4), scales=v_scales[:, 128:256], in_=v_grouped1[:].rearrange("p e t -> p (e t)"))
         total = held.tile([P, 1], F32, name="total")
         nc.scalar.activation(total[:], sums[0][:], IDENTITY, bias=sums[1][:])
-        inv = held.tile([P, 1], F32, name="inv")
+        inv = held.tile([P, 1], F32, name="inv", tag="v_raw1", align_bytes=64)
         nc.vector.reciprocal(inv[:], total[:])
 
         HV = DV // 2
@@ -182,4 +186,4 @@ def tile_attend_ring_alibi_kernel(tc, qT, kT, vT, vs, pos, slope, offs, out):
                 nc.scalar.activation(res[:], y[:], COPY, scale=inv[:])
             else:
                 nc.vector.tensor_scalar(res[:], y[:], inv[:], None, MULT)
-            nc.sync.dma_start(out=out[0][:, cols], in_=res[:])
+            (nc.scalar if h == 0 else nc.sync).dma_start(out=out[0][:, cols], in_=res[:])

@@ -6,6 +6,7 @@ from concourse.masks import make_identity
 NQ, D, N, T, DV = 128, 512, 512, 1024, 256
 P = 128
 LAST = P - 1
+H = N // 2
 FLOPS = 2 * NQ * N * (D + DV)
 
 F32 = mybir.dt.float32
@@ -27,40 +28,43 @@ def tile_attend_ring_alibi_kernel(tc, qT, kT, vT, vs, pos, slope, offs, out):
         held = ctx.enter_context(tc.tile_pool(name="held", bufs=1))
         psum = ctx.enter_context(tc.psum_pool(name="psum", bufs=1))
 
+        def tile(shape, dtype, name, tag=None):
+            return held.tile(shape, dtype, name=name, tag=tag or name, align_bytes=64)
+
         offsets = held.tile([P, N // 16], U16, name="offsets")
-        k_raw = [held.tile([P, 2, T], F32, name=f"k_raw{u}", tag=f"k_raw{u}", align_bytes=64) for u in range(2)]
-        v_raw = [held.tile([P, T], F32, name=f"v_raw{j}", tag=f"v_raw{j}", align_bytes=64) for j in range(2)]
-        q_raw = held.tile([P, 4, NQ], F32, name="q_raw", tag="v_round", align_bytes=64)
-        pos_pool = held.tile([P, T], F32, name="pos_pool")
-        vs_pool = held.tile([P, T], F32, name="vs_pool")
-        slope_col = held.tile([P, 1], F32, name="slope_col", tag="k_codes", align_bytes=64)
+        k_raw = [tile([P, 2, T], F32, f"k_raw{u}") for u in range(2)]
+        v_raw = [tile([P, T], F32, f"v_raw{j}") for j in range(2)]
+        q_raw = tile([P, 4, NQ], F32, "q_raw")
+        pos_pool = tile([P, T], F32, "pos_pool")
+        vs_pool = tile([P, T], F32, "vs_pool")
+        slope_rows = tile([P, P], F32, "slope_rows")
 
         k_rows = kT.rearrange("(p t) n -> p t n", t=4)
 
-        def load_cols(tile, rows, a, b):
-            nc.sync.dma_start(out=tile[:, :, a:b], in_=rows[:, :, a:b])
+        def load_keys(u, a, b):
+            nc.sync.dma_start(out=k_raw[u][:, :, a:b], in_=k_rows[:, 2 * u : 2 * u + 2, a:b])
 
         nc.vector.memset(pos_pool[0:LAST, :], 0.0)
         nc.vector.memset(vs_pool[0:LAST, :], 0.0)
+        nc.gpsimd.memset(slope_rows[0:LAST, :], 0.0)
         nc.sync.dma_start(offsets[:], offs)
-        load_cols(k_raw[0], k_rows[:, 0:2, :], 0, 512)
+        load_keys(0, 0, 512)
         nc.scalar.dma_start(out=pos_pool[LAST:P, :], in_=pos[0:1, :])
         nc.scalar.dma_start(out=vs_pool[LAST:P, :], in_=vs[0:1, :])
-        nc.scalar.dma_start(out=slope_col[:], in_=slope[0])
-        load_cols(k_raw[0], k_rows[:, 0:2, :], 512, T)
-        load_cols(k_raw[1], k_rows[:, 2:4, :], 0, 512)
-        load_cols(k_raw[1], k_rows[:, 2:4, :], 512, 768)
-        load_cols(k_raw[1], k_rows[:, 2:4, :], 768, T)
+        nc.scalar.dma_start(out=slope_rows[LAST:P, :], in_=slope[0].rearrange("q o -> o q"))
+        load_keys(0, 512, T)
+        load_keys(1, 0, 512)
+        load_keys(1, 512, T)
         nc.sync.dma_start(out=q_raw[:], in_=qT[0].rearrange("(p t) q -> p t q", t=4))
         for h in range(2):
             nc.sync.dma_start(out=v_raw[0][:, h * 512 : (h + 1) * 512], in_=vT[0:P, h * 512 : (h + 1) * 512])
         nc.sync.dma_start(out=v_raw[1][:], in_=vT[P : 2 * P, :])
 
-        warm = held.tile([P, 1], F32, name="warm")
-        warm_out = held.tile([P, 1], F32, name="warm_out")
+        warm = tile([P, 1], F32, "warm")
+        warm_out = tile([P, 1], F32, "warm_out")
         nc.vector.memset(warm[:], 0.0)
         nc.scalar.activation(warm_out[:], warm[:], EXP)
-        ident = held.tile([P, P], F32, name="ident")
+        ident = tile([P, P], F32, "ident")
         make_identity(nc, ident[:])
 
         def pair_up(engine, pairs, raw, a, b):
@@ -71,50 +75,46 @@ def tile_attend_ring_alibi_kernel(tc, qT, kT, vT, vs, pos, slope, offs, out):
             else:
                 nc.vector.tensor_copy(out=dst, in_=src)
 
-        def planes(name, width, tag):
-            codes = held.tile([P, width], U32, name=name + "_codes", tag=tag, align_bytes=64)
-            scales = held.tile([P, width], U8, name=name + "_scales", align_bytes=64)
-            return codes, scales
+        def planes(name, width, tag=None):
+            return tile([P, width], U32, name + "_codes", tag), tile([P, width], U8, name + "_scales")
 
-        pos_listed = held.tile([P, N], F32, name="pos_listed", tag="k_pairs1", align_bytes=64)
-        k_pairs = [held.tile([P, 2 * T], BF16, name="k_pairs0", align_bytes=64)]
-        vs_listed = held.tile([P, N], F32, name="vs_listed")
+        shared = tile([P, 2 * N + H], U32, "shared")
+        k_words = shared[:, 0 : 2 * N].rearrange("p (n u) -> p n u", u=2)
+        vs_listed = shared[:, 2 * N - H : 2 * N + H].bitcast(F32)
+
+        pos_listed = tile([P, N], F32, "pos_listed")
         nc.vector.tensor_copy(pos_listed[:], pos_pool[:].indirect(offsets[:]))
-        nc.vector.tensor_copy(vs_listed[:], vs_pool[:].indirect(offsets[:]))
-        pair_up("scalar", k_pairs[0], k_raw[0], 0, 512)
+        nc.vector.tensor_copy(vs_listed[:, H:N], vs_pool[:].indirect(offsets[:, 16:32]))
+        k_pairs0 = tile([P, 2 * T], BF16, "k_pairs0")
+        pair_up("scalar", k_pairs0, k_raw[0], 0, 512)
         pos_bank = psum.tile([P, 4, P], F32, name="pos_bank", tag="p0")
         for j in range(4):
             nc.tensor.transpose(pos_bank[:, j, :], pos_listed[:, j * P : (j + 1) * P], ident[:])
-        pos_cols = held.tile([P, 4], F32, name="pos_cols")
+        pos_cols = tile([P, 4], F32, "pos_cols")
         nc.scalar.copy(pos_cols[:], pos_bank[:, :, LAST])
         spread = psum.tile([P, N], F32, name="spread", tag="y0")
         for j in range(4):
             nc.tensor.transpose(spread[:, j * P : (j + 1) * P], pos_cols[:, j : j + 1].to_broadcast([P, P]), ident[:])
-        vs_bank = psum.tile([P, 4, P], F32, name="vs_bank", tag="p0")
-        for t in range(4):
-            nc.tensor.transpose(vs_bank[:, t, :], vs_listed[:, t : N : 4], ident[:])
+        slope_bank = psum.tile([P, P], F32, name="slope_bank", tag="p0")
+        nc.tensor.transpose(slope_bank[:], slope_rows[:], ident[:])
 
-        k_words = held.tile([P, N, 2], U32, name="k_words", align_bytes=64)
-        pair_up("vector", k_pairs[0], k_raw[0], 512, T)
-        nc.vector.tensor_copy(k_words[:, :, 0], k_pairs[0][:].bitcast(U32).indirect(offsets[:]))
-        k_pairs.append(held.tile([P, 2 * T], BF16, name="k_pairs1", tag="k_pairs1", align_bytes=64))
-        pair_up("scalar", k_pairs[1], k_raw[1], 0, 512)
-        pair_up("vector", k_pairs[1], k_raw[1], 512, 768)
-        pair_up("scalar", k_pairs[1], k_raw[1], 768, 832)
-        pair_up("vector", k_pairs[1], k_raw[1], 832, T)
-        for h in range(2):
-            nc.vector.tensor_copy(k_words[:, h * 256 : (h + 1) * 256, 1], k_pairs[1][:].bitcast(U32).indirect(offsets[:, h * 16 : (h + 1) * 16]))
-        bias = held.tile([P, 4, P], F32, name="bias", tag="k_raw1", align_bytes=64)
-        nc.scalar.activation(bias[:], spread[:].rearrange("p (i t) -> p t i", t=4), COPY, scale=slope_col[:])
-        q_grouped = held.tile([P, NQ, 4], BF16, name="q_grouped", tag="k_codes", align_bytes=64)
+        pair_up("vector", k_pairs0, k_raw[0], 512, T)
+        nc.vector.tensor_copy(k_words[:, :, 0], k_pairs0[:].bitcast(U32).indirect(offsets[:]))
+        k_pairs1 = tile([P, 2 * T], BF16, "k_pairs1", "pos_listed")
+        pair_up("scalar", k_pairs1, k_raw[1], 0, 512)
+        pair_up("scalar", k_pairs1, k_raw[1], 512, 640)
+        pair_up("vector", k_pairs1, k_raw[1], 640, T)
+        nc.vector.tensor_copy(k_words[:, :, 1], k_pairs1[:].bitcast(U32).indirect(offsets[:]))
+        q_grouped = tile([P, NQ, 4], BF16, "q_grouped", "k_raw1")
         nc.scalar.activation(q_grouped[:], q_raw[:].rearrange("p t q -> p q t"), COPY)
-        vs_cols = held.tile([P, 4], F32, name="vs_cols", tag="k_pairs1", align_bytes=64)
-        nc.vector.tensor_copy(vs_cols[:], vs_bank[:, :, LAST])
-        q_codes, q_scales = planes("q", NQ, "q_codes")
+        slope_col = tile([P, 1], F32, "slope_col", "k_raw0")
+        nc.scalar.copy(slope_col[:], slope_bank[:, LAST:P])
+        bias = tile([P, 4, P], F32, "bias", "q_raw")
+        nc.scalar.activation(bias[:], spread[:].rearrange("p (i t) -> p t i", t=4), COPY, scale=slope_col[:])
+        q_codes, q_scales = planes("q", NQ)
         nc.vector.quantize_mx(out=q_codes[:].bitcast(FP8X4), scales=q_scales[:], in_=q_grouped[:].rearrange("p q t -> p (q t)"))
-        k_codes, k_scales = planes("k", N, "k_codes")
-        k_flat = k_words[:].rearrange("p n u -> p (n u)").bitcast(BF16)
-        H = N // 2
+        k_codes, k_scales = planes("k", N, "k_raw1")
+        k_flat = shared[:, 0 : 2 * N].bitcast(BF16)
         scores = []
         for h in range(2):
             cols = slice(h * H, (h + 1) * H)
@@ -122,58 +122,64 @@ def tile_attend_ring_alibi_kernel(tc, qT, kT, vT, vs, pos, slope, offs, out):
             bank = psum.tile([P, H], F32, name=f"scores{h}", tag=f"scores{h}")
             nc.tensor.matmul_mx(out=bank[:], lhsT=q_codes[:].bitcast(FP8X4), lhsT_scale=q_scales[:], rhs=k_codes[:, cols].bitcast(FP8X4), rhs_scale=k_scales[:, cols], start=True, stop=True)
             scores.append(bank)
+        nc.vector.tensor_copy(vs_listed[:, 0:H], vs_pool[:].indirect(offsets[:, 0:16]))
+        vs_bank = psum.tile([P, 4, P], F32, name="vs_bank", tag="p1")
+        for t in range(4):
+            nc.tensor.transpose(vs_bank[:, t, :], vs_listed[:, t : N : 4], ident[:])
 
-        v_round = held.tile([P, T], BF16, name="v_round", tag="v_round", align_bytes=64)
+        v_round = tile([P, T], BF16, "v_round", "k_raw0")
         for h in range(2):
             nc.scalar.activation(v_round[:, h * 512 : (h + 1) * 512], v_raw[0][:, h * 512 : (h + 1) * 512], COPY)
-        v_listed0 = held.tile([P, 2, P, 2], BF16, name="v_listed0", tag="v_listed0", align_bytes=64)
+        v_listed0 = tile([P, 2, P, 2], BF16, "v_listed0")
         nc.scalar.activation(v_listed0[:].rearrange("p u s e -> p s u e"), v_round[:].indirect(offsets[:]), COPY)
+        vs_cols = tile([P, 4], F32, "vs_cols", "k_raw0")
+        nc.scalar.copy(vs_cols[:], vs_bank[:, :, LAST])
 
-        s = held.tile([P, 4, P], F32, name="s", tag="s", align_bytes=64)
+        s = tile([P, 4, P], F32, "s")
         for h in range(2):
             part = slice(h * 64, (h + 1) * 64)
             nc.vector.tensor_tensor(s[:, :, part], scores[h][:].rearrange("p (i t) -> p t i", t=4), bias[:, :, part], ADD)
-        minus_m = held.tile([P, 1], F32, name="minus_m")
+        minus_m = tile([P, 1], F32, "minus_m")
         nc.vector.tensor_reduce(out=minus_m[:], in_=s[:].rearrange("p t i -> p (t i)"), axis=X, op=MAX, negate=True)
 
         p_banks, sums = [], []
         for u in range(2):
-            pu = held.tile([P, 2, P], F32, name=f"p{u}", tag="v_round" if u == 0 else "p1", align_bytes=64)
-            su = held.tile([P, 1], F32, name=f"sum{u}")
+            pu = tile([P, 2, P], F32, f"p{u}", "v_raw0" if u == 0 else None)
+            su = tile([P, 1], F32, f"sum{u}")
             nc.scalar.activation(pu[:], s[:, 2 * u : 2 * u + 2, :], EXP, bias=minus_m[:], accum_out=su[:])
             bank = psum.tile([P, 2, P], F32, name=f"p_bank{u}", tag=f"p{u}")
             for e in range(2):
                 nc.tensor.transpose(bank[:, e, :], pu[:, e, :], ident[:])
             p_banks.append(bank)
             sums.append(su)
+        total = tile([P, 1], F32, "total")
+        nc.scalar.activation(total[:], sums[0][:], IDENTITY, bias=sums[1][:])
 
-        v_codes, v_scales = planes("v", DV, "k_pairs1")
+        v_codes, v_scales = planes("v", DV, "k_raw0")
 
-        def turn_values(j, halves, tag):
-            bank = psum.tile([P, 2, P], F32, name=f"v_bank{j}", tag=tag)
+        def turn_values(j, halves, bank_tag, tag):
+            bank = psum.tile([P, 2, P], F32, name=f"v_bank{j}", tag=bank_tag)
             for u in range(2):
                 nc.tensor.transpose(bank[:, u, :], halves[u], ident[:])
-            grouped = held.tile([P, P, 4], BF16, name=f"v_grouped{j}", tag="s" if j == 0 else "v_grouped1", align_bytes=64)
+            grouped = tile([P, P, 4], BF16, f"v_grouped{j}", tag)
             words = grouped[:].rearrange("p e t -> p (e t)").bitcast(F32).rearrange("p (e u) -> p e u", u=2)
             nc.scalar.copy(words, bank[:].rearrange("p u e -> p e u"))
             return grouped
 
-        v_grouped0 = turn_values(0, [v_listed0[:, u, :, :].rearrange("p s e -> p (s e)").bitcast(F32) for u in range(2)], "v_bank0")
-        v_listed1 = held.tile([P, N], BF16, name="v_listed1", tag="k_raw1", align_bytes=64)
+        v_grouped0 = turn_values(0, [v_listed0[:, u, :, :].rearrange("p s e -> p (s e)").bitcast(F32) for u in range(2)], "v_bank0", "s")
+        v_listed1 = tile([P, N], BF16, "v_listed1", "q_raw")
         nc.vector.tensor_copy(v_listed1[:], v_raw[1][:].indirect(offsets[:]))
 
-        w_grouped = held.tile([P, NQ, 4], BF16, name="w_grouped", tag="v_raw1", align_bytes=64)
+        w_grouped = tile([P, NQ, 4], BF16, "w_grouped", "v_raw1")
         for u in range(2):
             pair = slice(2 * u, 2 * u + 2)
             nc.vector.tensor_tensor(w_grouped[:, :, pair], p_banks[u][:].rearrange("p e q -> p q e"), vs_cols[:, pair].unsqueeze(1).to_broadcast([P, NQ, 2]), MULT)
-        v_grouped1 = turn_values(1, [v_listed1[:].bitcast(F32)[:, u : N // 2 : 2] for u in range(2)], "p0")
+        v_grouped1 = turn_values(1, [v_listed1[:].bitcast(F32)[:, u : N // 2 : 2] for u in range(2)], "p0", None)
         nc.vector.quantize_mx(out=v_codes[:, 0:128].bitcast(FP8X4), scales=v_scales[:, 0:128], in_=v_grouped0[:].rearrange("p e t -> p (e t)"))
-        w_codes, w_scales = planes("w", NQ, "w_codes")
+        w_codes, w_scales = planes("w", NQ)
         nc.vector.quantize_mx(out=w_codes[:].bitcast(FP8X4), scales=w_scales[:], in_=w_grouped[:].rearrange("p q t -> p (q t)"))
         nc.vector.quantize_mx(out=v_codes[:, 128:256].bitcast(FP8X4), scales=v_scales[:, 128:256], in_=v_grouped1[:].rearrange("p e t -> p (e t)"))
-        total = held.tile([P, 1], F32, name="total")
-        nc.scalar.activation(total[:], sums[0][:], IDENTITY, bias=sums[1][:])
-        inv = held.tile([P, 1], F32, name="inv", tag="v_raw1", align_bytes=64)
+        inv = tile([P, 1], F32, "inv", "v_raw1")
         nc.vector.reciprocal(inv[:], total[:])
 
         HV = DV // 2
@@ -181,9 +187,9 @@ def tile_attend_ring_alibi_kernel(tc, qT, kT, vT, vs, pos, slope, offs, out):
             cols = slice(h * HV, (h + 1) * HV)
             y = psum.tile([P, HV], F32, name=f"y{h}", tag="y0" if h == 0 else "scores0")
             nc.tensor.matmul_mx(out=y[:], lhsT=w_codes[:].bitcast(FP8X4), lhsT_scale=w_scales[:], rhs=v_codes[:, cols].bitcast(FP8X4), rhs_scale=v_scales[:, cols], start=True, stop=True)
-            res = held.tile([P, HV], F32, name=f"res{h}")
+            res = tile([P, HV], F32, f"res{h}")
             if h == 0:
                 nc.scalar.activation(res[:], y[:], COPY, scale=inv[:])
             else:
                 nc.vector.tensor_scalar(res[:], y[:], inv[:], None, MULT)
-            (nc.scalar if h == 0 else nc.sync).dma_start(out=out[0][:, cols], in_=res[:])
+            nc.sync.dma_start(out=out[0][:, cols], in_=res[:])

@@ -130,8 +130,8 @@ def tile_attend_ring_alibi_kernel(tc, qT, kT, vT, vs, pos, slope, offs, out):
         v_round = tile([P, T], BF16, "v_round", "k_raw0")
         for h in range(2):
             nc.scalar.activation(v_round[:, h * 512 : (h + 1) * 512], v_raw[0][:, h * 512 : (h + 1) * 512], COPY)
-        v_listed0 = tile([P, 2, P, 2], BF16, "v_listed0")
-        nc.scalar.activation(v_listed0[:].rearrange("p u s e -> p s u e"), v_round[:].indirect(offsets[:]), COPY)
+        v_listed0 = tile([P, N], BF16, "v_listed0")
+        nc.scalar.activation(v_listed0[:], v_round[:].indirect(offsets[:]), COPY)
         vs_cols = tile([P, 4], F32, "vs_cols", "k_raw0")
         nc.scalar.copy(vs_cols[:], vs_bank[:, :, LAST])
 
@@ -166,7 +166,7 @@ def tile_attend_ring_alibi_kernel(tc, qT, kT, vT, vs, pos, slope, offs, out):
             nc.scalar.copy(words, bank[:].rearrange("p u e -> p e u"))
             return grouped
 
-        v_grouped0 = turn_values(0, [v_listed0[:, u, :, :].rearrange("p s e -> p (s e)").bitcast(F32) for u in range(2)], "v_bank0", "s")
+        v_grouped0 = turn_values(0, [v_listed0[:].bitcast(F32)[:, u : N // 2 : 2] for u in range(2)], "v_bank0", "s")
         v_listed1 = tile([P, N], BF16, "v_listed1", "q_raw")
         nc.vector.tensor_copy(v_listed1[:], v_raw[1][:].indirect(offsets[:]))
 

@@ -26,15 +26,20 @@ def tile_attend_ring_alibi_kernel(tc, qT, kT, vT, vs, pos, slope, offs, out):
     nc = tc.nc
     with ExitStack() as ctx:
         held = ctx.enter_context(tc.tile_pool(name="held", bufs=1))
+        reuse = ctx.enter_context(tc.tile_pool(name="reuse", bufs=1))
         psum = ctx.enter_context(tc.psum_pool(name="psum", bufs=1))
 
         def tile(shape, dtype, name, tag=None):
             return held.tile(shape, dtype, name=name, tag=tag or name, align_bytes=64)
 
+        def tile_at(offset, shape, dtype, name):
+            return reuse.tile(shape, dtype, name=name, align_bytes=64, offset=offset)
+
+        AT_K, AT_Q, AT_V = 0, 8192, 11264
         offsets = held.tile([P, N // 16], U16, name="offsets")
-        k_raw = [tile([P, 2, T], F32, f"k_raw{u}") for u in range(2)]
-        v_raw = [tile([P, T], F32, f"v_raw{j}") for j in range(2)]
-        q_raw = tile([P, 4, NQ], F32, "q_raw")
+        k_raw = [tile([P, 2, T], F32, "k_raw0"), tile_at(AT_K, [P, 2, T], F32, "k_raw1")]
+        v_raw = [tile_at(AT_V, [P, T], F32, "v_raw0"), tile([P, T], F32, "v_raw1")]
+        q_raw = tile_at(AT_Q, [P, 4, NQ], F32, "q_raw")
         pos_pool = tile([P, T], F32, "pos_pool")
         vs_pool = tile([P, T], F32, "vs_pool")
         slope_rows = tile([P, P], F32, "slope_rows")
@@ -75,16 +80,16 @@ def tile_attend_ring_alibi_kernel(tc, qT, kT, vT, vs, pos, slope, offs, out):
             else:
                 nc.vector.tensor_copy(out=dst, in_=src)
 
-        def planes(name, width, tag=None):
-            return tile([P, width], U32, name + "_codes", tag), tile([P, width], U8, name + "_scales")
+        def planes(name, width):
+            return tile([P, width], U32, name + "_codes"), tile([P, width], U8, name + "_scales")
 
         shared = tile([P, 2 * N + H], U32, "shared")
-        k_words = shared[:, 0 : 2 * N].rearrange("p (n u) -> p n u", u=2)
-        vs_listed = shared[:, 2 * N - H : 2 * N + H].bitcast(F32)
+        k_words = shared[:, H : 2 * N + H].rearrange("p (n u) -> p n u", u=2)
+        vs_listed = shared[:, 0:N].bitcast(F32)
 
         pos_listed = tile([P, N], F32, "pos_listed")
         nc.vector.tensor_copy(pos_listed[:], pos_pool[:].indirect(offsets[:]))
-        nc.vector.tensor_copy(vs_listed[:, H:N], vs_pool[:].indirect(offsets[:, 16:32]))
+        nc.vector.tensor_copy(vs_listed[:, 0:H], vs_pool[:].indirect(offsets[:, 0:16]))
         k_pairs0 = tile([P, 2 * T], BF16, "k_pairs0")
         pair_up("scalar", k_pairs0, k_raw[0], 0, 512)
         pos_bank = psum.tile([P, 4, P], F32, name="pos_bank", tag="p0")
@@ -95,7 +100,7 @@ def tile_attend_ring_alibi_kernel(tc, qT, kT, vT, vs, pos, slope, offs, out):
         spread = psum.tile([P, N], F32, name="spread", tag="y0")
         for j in range(4):
             nc.tensor.transpose(spread[:, j * P : (j + 1) * P], pos_cols[:, j : j + 1].to_broadcast([P, P]), ident[:])
-        slope_bank = psum.tile([P, P], F32, name="slope_bank", tag="p0")
+        slope_bank = psum.tile([P, P], F32, name="slope_bank", tag="v_bank")
         nc.tensor.transpose(slope_bank[:], slope_rows[:], ident[:])
 
         pair_up("vector", k_pairs0, k_raw[0], 512, T)
@@ -105,16 +110,16 @@ def tile_attend_ring_alibi_kernel(tc, qT, kT, vT, vs, pos, slope, offs, out):
         pair_up("scalar", k_pairs1, k_raw[1], 512, 640)
         pair_up("vector", k_pairs1, k_raw[1], 640, T)
         nc.vector.tensor_copy(k_words[:, :, 1], k_pairs1[:].bitcast(U32).indirect(offsets[:]))
-        q_grouped = tile([P, NQ, 4], BF16, "q_grouped", "k_raw1")
-        nc.scalar.activation(q_grouped[:], q_raw[:].rearrange("p t q -> p q t"), COPY)
-        slope_col = tile([P, 1], F32, "slope_col", "k_raw0")
+        slope_col = tile_at(AT_K, [P, 1], F32, "slope_col")
         nc.scalar.copy(slope_col[:], slope_bank[:, LAST:P])
-        bias = tile([P, 4, P], F32, "bias", "q_raw")
+        q_grouped = tile_at(AT_K + 64, [P, NQ, 4], BF16, "q_grouped")
+        nc.scalar.activation(q_grouped[:], q_raw[:].rearrange("p t q -> p q t"), COPY)
+        bias = tile_at(AT_K + 2048, [P, 4, P], F32, "bias")
         nc.scalar.activation(bias[:], spread[:].rearrange("p (i t) -> p t i", t=4), COPY, scale=slope_col[:])
         q_codes, q_scales = planes("q", NQ)
         nc.vector.quantize_mx(out=q_codes[:].bitcast(FP8X4), scales=q_scales[:], in_=q_grouped[:].rearrange("p q t -> p (q t)"))
-        k_codes, k_scales = planes("k", N, "k_raw1")
-        k_flat = shared[:, 0 : 2 * N].bitcast(BF16)
+        k_codes, k_scales = tile([P, N], U32, "k_codes"), tile_at(AT_Q, [P, N], U8, "k_scales")
+        k_flat = shared[:, H : 2 * N + H].bitcast(BF16)
         scores = []
         for h in range(2):
             cols = slice(h * H, (h + 1) * H)
@@ -122,17 +127,17 @@ def tile_attend_ring_alibi_kernel(tc, qT, kT, vT, vs, pos, slope, offs, out):
             bank = psum.tile([P, H], F32, name=f"scores{h}", tag=f"scores{h}")
             nc.tensor.matmul_mx(out=bank[:], lhsT=q_codes[:].bitcast(FP8X4), lhsT_scale=q_scales[:], rhs=k_codes[:, cols].bitcast(FP8X4), rhs_scale=k_scales[:, cols], start=True, stop=True)
             scores.append(bank)
-        nc.vector.tensor_copy(vs_listed[:, 0:H], vs_pool[:].indirect(offsets[:, 0:16]))
+        nc.vector.tensor_copy(vs_listed[:, H:N], vs_pool[:].indirect(offsets[:, 16:32]))
         vs_bank = psum.tile([P, 4, P], F32, name="vs_bank", tag="p1")
         for t in range(4):
             nc.tensor.transpose(vs_bank[:, t, :], vs_listed[:, t : N : 4], ident[:])
 
-        v_round = tile([P, T], BF16, "v_round", "k_raw0")
+        v_round = tile_at(AT_Q + 512, [P, T], BF16, "v_round")
         for h in range(2):
             nc.scalar.activation(v_round[:, h * 512 : (h + 1) * 512], v_raw[0][:, h * 512 : (h + 1) * 512], COPY)
         v_listed0 = tile([P, N], BF16, "v_listed0")
         nc.scalar.activation(v_listed0[:], v_round[:].indirect(offsets[:]), COPY)
-        vs_cols = tile([P, 4], F32, "vs_cols", "k_raw0")
+        vs_cols = tile_at(AT_V + 1024, [P, 4], F32, "vs_cols")
         nc.scalar.copy(vs_cols[:], vs_bank[:, :, LAST])
 
         s = tile([P, 4, P], F32, "s")
@@ -144,7 +149,7 @@ def tile_attend_ring_alibi_kernel(tc, qT, kT, vT, vs, pos, slope, offs, out):
 
         p_banks, sums = [], []
         for u in range(2):
-            pu = tile([P, 2, P], F32, f"p{u}", "v_raw0" if u == 0 else None)
+            pu = tile_at(AT_V, [P, 2, P], F32, "p0") if u == 0 else tile([P, 2, P], F32, "p1")
             su = tile([P, 1], F32, f"sum{u}")
             nc.scalar.activation(pu[:], s[:, 2 * u : 2 * u + 2, :], EXP, bias=minus_m[:], accum_out=su[:])
             bank = psum.tile([P, 2, P], F32, name=f"p_bank{u}", tag=f"p{u}")
@@ -152,34 +157,33 @@ def tile_attend_ring_alibi_kernel(tc, qT, kT, vT, vs, pos, slope, offs, out):
                 nc.tensor.transpose(bank[:, e, :], pu[:, e, :], ident[:])
             p_banks.append(bank)
             sums.append(su)
-        total = tile([P, 1], F32, "total")
-        nc.scalar.activation(total[:], sums[0][:], IDENTITY, bias=sums[1][:])
 
-        v_codes, v_scales = planes("v", DV, "k_raw0")
+        v_codes, v_scales = planes("v", DV)
 
-        def turn_values(j, halves, bank_tag, tag):
-            bank = psum.tile([P, 2, P], F32, name=f"v_bank{j}", tag=bank_tag)
+        def turn_values(j, halves, grouped):
+            bank = psum.tile([P, 2, P], F32, name=f"v_bank{j}", tag="v_bank")
             for u in range(2):
                 nc.tensor.transpose(bank[:, u, :], halves[u], ident[:])
-            grouped = tile([P, P, 4], BF16, f"v_grouped{j}", tag)
             words = grouped[:].rearrange("p e t -> p (e t)").bitcast(F32).rearrange("p (e u) -> p e u", u=2)
             nc.scalar.copy(words, bank[:].rearrange("p u e -> p e u"))
             return grouped
 
-        v_grouped0 = turn_values(0, [v_listed0[:].bitcast(F32)[:, u : N // 2 : 2] for u in range(2)], "v_bank0", "s")
-        v_listed1 = tile([P, N], BF16, "v_listed1", "q_raw")
+        v_grouped0 = turn_values(0, [v_listed0[:].bitcast(F32)[:, u : N // 2 : 2] for u in range(2)], tile_at(AT_V, [P, P, 4], BF16, "v_grouped0"))
+        total = tile([P, 1], F32, "total")
+        nc.scalar.activation(total[:], sums[0][:], IDENTITY, bias=sums[1][:])
+        v_listed1 = tile_at(AT_K + 2048, [P, N], BF16, "v_listed1")
         nc.vector.tensor_copy(v_listed1[:], v_raw[1][:].indirect(offsets[:]))
 
-        w_grouped = tile([P, NQ, 4], BF16, "w_grouped", "v_raw1")
+        w_grouped = tile([P, NQ, 4], BF16, "w_grouped")
         for u in range(2):
             pair = slice(2 * u, 2 * u + 2)
             nc.vector.tensor_tensor(w_grouped[:, :, pair], p_banks[u][:].rearrange("p e q -> p q e"), vs_cols[:, pair].unsqueeze(1).to_broadcast([P, NQ, 2]), MULT)
-        v_grouped1 = turn_values(1, [v_listed1[:].bitcast(F32)[:, u : N // 2 : 2] for u in range(2)], "p0", None)
+        v_grouped1 = turn_values(1, [v_listed1[:].bitcast(F32)[:, u : N // 2 : 2] for u in range(2)], tile([P, P, 4], BF16, "v_grouped1"))
         nc.vector.quantize_mx(out=v_codes[:, 0:128].bitcast(FP8X4), scales=v_scales[:, 0:128], in_=v_grouped0[:].rearrange("p e t -> p (e t)"))
         w_codes, w_scales = planes("w", NQ)
         nc.vector.quantize_mx(out=w_codes[:].bitcast(FP8X4), scales=w_scales[:], in_=w_grouped[:].rearrange("p q t -> p (q t)"))
         nc.vector.quantize_mx(out=v_codes[:, 128:256].bitcast(FP8X4), scales=v_scales[:, 128:256], in_=v_grouped1[:].rearrange("p e t -> p (e t)"))
-        inv = tile([P, 1], F32, "inv", "v_raw1")
+        inv = tile([P, 1], F32, "inv")
         nc.vector.reciprocal(inv[:], total[:])
 
         HV = DV // 2

@@ -83,13 +83,12 @@ def tile_attend_ring_alibi_kernel(tc, qT, kT, vT, vs, pos, slope, offs, out):
         def planes(name, width):
             return tile([P, width], U32, name + "_codes"), tile([P, width], U8, name + "_scales")
 
-        shared = tile([P, 2 * N + H], U32, "shared")
-        k_words = shared[:, H : 2 * N + H].rearrange("p (n u) -> p n u", u=2)
-        vs_listed = shared[:, 0:N].bitcast(F32)
+        k_words = tile([P, N, 2], U32, "k_words")
+        vs_listed = tile([P, 4, P], F32, "vs_listed")
 
         pos_listed = tile([P, N], F32, "pos_listed")
         nc.vector.tensor_copy(pos_listed[:], pos_pool[:].indirect(offsets[:]))
-        nc.vector.tensor_copy(vs_listed[:, 0:H], vs_pool[:].indirect(offsets[:, 0:16]))
+        nc.vector.tensor_copy(vs_listed[:].bitcast(U32).rearrange("p t s -> p s t"), vs_pool[:].bitcast(U32).indirect(offsets[:]))
         k_pairs0 = tile([P, 2 * T], BF16, "k_pairs0")
         pair_up("scalar", k_pairs0, k_raw[0], 0, 512)
         pos_bank = psum.tile([P, 4, P], F32, name="pos_bank", tag="p0")
@@ -102,24 +101,30 @@ def tile_attend_ring_alibi_kernel(tc, qT, kT, vT, vs, pos, slope, offs, out):
             nc.tensor.transpose(spread[:, j * P : (j + 1) * P], pos_cols[:, j : j + 1].to_broadcast([P, P]), ident[:])
         slope_bank = psum.tile([P, P], F32, name="slope_bank", tag="v_bank")
         nc.tensor.transpose(slope_bank[:], slope_rows[:], ident[:])
+        vs_bank = psum.tile([P, 4, P], F32, name="vs_bank", tag="p0")
+        for t in range(4):
+            nc.tensor.transpose(vs_bank[:, t, :], vs_listed[:, t, :], ident[:])
 
-        pair_up("vector", k_pairs0, k_raw[0], 512, T)
+        pair_up("scalar", k_pairs0, k_raw[0], 512, 704)
+        pair_up("vector", k_pairs0, k_raw[0], 704, T)
         nc.vector.tensor_copy(k_words[:, :, 0], k_pairs0[:].bitcast(U32).indirect(offsets[:]))
         k_pairs1 = tile([P, 2 * T], BF16, "k_pairs1", "pos_listed")
         pair_up("scalar", k_pairs1, k_raw[1], 0, 512)
-        pair_up("scalar", k_pairs1, k_raw[1], 512, 640)
-        pair_up("vector", k_pairs1, k_raw[1], 640, T)
+        pair_up("scalar", k_pairs1, k_raw[1], 512, 704)
+        pair_up("vector", k_pairs1, k_raw[1], 704, T)
         nc.vector.tensor_copy(k_words[:, :, 1], k_pairs1[:].bitcast(U32).indirect(offsets[:]))
         slope_col = tile_at(AT_K, [P, 1], F32, "slope_col")
         nc.scalar.copy(slope_col[:], slope_bank[:, LAST:P])
         q_grouped = tile_at(AT_K + 64, [P, NQ, 4], BF16, "q_grouped")
         nc.scalar.activation(q_grouped[:], q_raw[:].rearrange("p t q -> p q t"), COPY)
+        vs_cols = tile_at(AT_K + 4096, [P, 4], F32, "vs_cols")
+        nc.scalar.copy(vs_cols[:], vs_bank[:, :, LAST])
         bias = tile_at(AT_K + 2048, [P, 4, P], F32, "bias")
         nc.scalar.activation(bias[:], spread[:].rearrange("p (i t) -> p t i", t=4), COPY, scale=slope_col[:])
         q_codes, q_scales = planes("q", NQ)
         nc.vector.quantize_mx(out=q_codes[:].bitcast(FP8X4), scales=q_scales[:], in_=q_grouped[:].rearrange("p q t -> p (q t)"))
         k_codes, k_scales = tile([P, N], U32, "k_codes"), tile_at(AT_Q, [P, N], U8, "k_scales")
-        k_flat = shared[:, H : 2 * N + H].bitcast(BF16)
+        k_flat = k_words[:].rearrange("p n u -> p (n u)").bitcast(BF16)
         scores = []
         for h in range(2):
             cols = slice(h * H, (h + 1) * H)
@@ -127,18 +132,12 @@ def tile_attend_ring_alibi_kernel(tc, qT, kT, vT, vs, pos, slope, offs, out):
             bank = psum.tile([P, H], F32, name=f"scores{h}", tag=f"scores{h}")
             nc.tensor.matmul_mx(out=bank[:], lhsT=q_codes[:].bitcast(FP8X4), lhsT_scale=q_scales[:], rhs=k_codes[:, cols].bitcast(FP8X4), rhs_scale=k_scales[:, cols], start=True, stop=True)
             scores.append(bank)
-        nc.vector.tensor_copy(vs_listed[:, H:N], vs_pool[:].indirect(offsets[:, 16:32]))
-        vs_bank = psum.tile([P, 4, P], F32, name="vs_bank", tag="p1")
-        for t in range(4):
-            nc.tensor.transpose(vs_bank[:, t, :], vs_listed[:, t : N : 4], ident[:])
 
         v_round = tile_at(AT_Q + 512, [P, T], BF16, "v_round")
         for h in range(2):
             nc.scalar.activation(v_round[:, h * 512 : (h + 1) * 512], v_raw[0][:, h * 512 : (h + 1) * 512], COPY)
         v_listed0 = tile([P, N], BF16, "v_listed0")
         nc.scalar.activation(v_listed0[:], v_round[:].indirect(offsets[:]), COPY)
-        vs_cols = tile_at(AT_V + 1024, [P, 4], F32, "vs_cols")
-        nc.scalar.copy(vs_cols[:], vs_bank[:, :, LAST])
 
         s = tile([P, 4, P], F32, "s")
         for h in range(2):
@@ -147,15 +146,14 @@ def tile_attend_ring_alibi_kernel(tc, qT, kT, vT, vs, pos, slope, offs, out):
         minus_m = tile([P, 1], F32, "minus_m")
         nc.vector.tensor_reduce(out=minus_m[:], in_=s[:].rearrange("p t i -> p (t i)"), axis=X, op=MAX, negate=True)
 
-        p_banks, sums = [], []
+        p_bank = psum.tile([P, 4, P], F32, name="p_bank", tag="p0")
+        sums = []
         for u in range(2):
             pu = tile_at(AT_V, [P, 2, P], F32, "p0") if u == 0 else tile([P, 2, P], F32, "p1")
             su = tile([P, 1], F32, f"sum{u}")
             nc.scalar.activation(pu[:], s[:, 2 * u : 2 * u + 2, :], EXP, bias=minus_m[:], accum_out=su[:])
-            bank = psum.tile([P, 2, P], F32, name=f"p_bank{u}", tag=f"p{u}")
             for e in range(2):
-                nc.tensor.transpose(bank[:, e, :], pu[:, e, :], ident[:])
-            p_banks.append(bank)
+                nc.tensor.transpose(p_bank[:, 2 * u + e, :], pu[:, e, :], ident[:])
             sums.append(su)
 
         v_codes, v_scales = planes("v", DV)
@@ -175,9 +173,7 @@ def tile_attend_ring_alibi_kernel(tc, qT, kT, vT, vs, pos, slope, offs, out):
         nc.vector.tensor_copy(v_listed1[:], v_raw[1][:].indirect(offsets[:]))
 
         w_grouped = tile([P, NQ, 4], BF16, "w_grouped")
-        for u in range(2):
-            pair = slice(2 * u, 2 * u + 2)
-            nc.vector.tensor_tensor(w_grouped[:, :, pair], p_banks[u][:].rearrange("p e q -> p q e"), vs_cols[:, pair].unsqueeze(1).to_broadcast([P, NQ, 2]), MULT)
+        nc.vector.tensor_tensor(w_grouped[:], p_bank[:].rearrange("p t q -> p q t"), vs_cols[:].unsqueeze(1).to_broadcast([P, NQ, 4]), MULT)
         v_grouped1 = turn_values(1, [v_listed1[:].bitcast(F32)[:, u : N // 2 : 2] for u in range(2)], tile([P, P, 4], BF16, "v_grouped1"))
         nc.vector.quantize_mx(out=v_codes[:, 0:128].bitcast(FP8X4), scales=v_scales[:, 0:128], in_=v_grouped0[:].rearrange("p e t -> p (e t)"))
         w_codes, w_scales = planes("w", NQ)

@@ -50,7 +50,7 @@ def tile_attend_ring_alibi_kernel(tc, qT, kT, vT, vs, pos, slope, offs, out):
             nc.sync.dma_start(out=k_raw[u][:, :, a:b], in_=k_rows[:, 2 * u : 2 * u + 2, a:b])
 
         nc.vector.memset(pos_pool[0:LAST, :], 0.0)
-        nc.vector.memset(vs_pool[0:LAST, :], 0.0)
+        nc.gpsimd.memset(vs_pool[0:LAST, :], 0.0)
         nc.gpsimd.memset(slope_rows[0:LAST, :], 0.0)
         nc.sync.dma_start(offsets[:], offs)
         load_keys(0, 0, 512)
@@ -83,12 +83,17 @@ def tile_attend_ring_alibi_kernel(tc, qT, kT, vT, vs, pos, slope, offs, out):
         def planes(name, width):
             return tile([P, width], U32, name + "_codes"), tile([P, width], U8, name + "_scales")
 
-        k_words = tile([P, N, 2], U32, "k_words")
-        vs_listed = tile([P, 4, P], F32, "vs_listed")
+        K0 = N - 64
+        shared = tile([P, K0 + 2 * N], U32, "shared")
+        k_words = shared[:, K0 : K0 + 2 * N].rearrange("p (n u) -> p n u", u=2)
+        vs_dealt = shared[:, 0:N].rearrange("p (t s) -> p t s", t=4)
+
+        def gather_scales(h):
+            nc.vector.tensor_copy(vs_dealt[:, :, h * 64 : (h + 1) * 64].rearrange("p t s -> p s t"), vs_pool[:].bitcast(U32).indirect(offsets[:, h * 16 : (h + 1) * 16]))
 
         pos_listed = tile([P, N], F32, "pos_listed")
         nc.vector.tensor_copy(pos_listed[:], pos_pool[:].indirect(offsets[:]))
-        nc.vector.tensor_copy(vs_listed[:].bitcast(U32).rearrange("p t s -> p s t"), vs_pool[:].bitcast(U32).indirect(offsets[:]))
+        gather_scales(0)
         k_pairs0 = tile([P, 2 * T], BF16, "k_pairs0")
         pair_up("scalar", k_pairs0, k_raw[0], 0, 512)
         pos_bank = psum.tile([P, 4, P], F32, name="pos_bank", tag="p0")
@@ -101,9 +106,6 @@ def tile_attend_ring_alibi_kernel(tc, qT, kT, vT, vs, pos, slope, offs, out):
             nc.tensor.transpose(spread[:, j * P : (j + 1) * P], pos_cols[:, j : j + 1].to_broadcast([P, P]), ident[:])
         slope_bank = psum.tile([P, P], F32, name="slope_bank", tag="v_bank")
         nc.tensor.transpose(slope_bank[:], slope_rows[:], ident[:])
-        vs_bank = psum.tile([P, 4, P], F32, name="vs_bank", tag="p0")
-        for t in range(4):
-            nc.tensor.transpose(vs_bank[:, t, :], vs_listed[:, t, :], ident[:])
 
         pair_up("scalar", k_pairs0, k_raw[0], 512, 704)
         pair_up("vector", k_pairs0, k_raw[0], 704, T)
@@ -117,14 +119,12 @@ def tile_attend_ring_alibi_kernel(tc, qT, kT, vT, vs, pos, slope, offs, out):
         nc.scalar.copy(slope_col[:], slope_bank[:, LAST:P])
         q_grouped = tile_at(AT_K + 64, [P, NQ, 4], BF16, "q_grouped")
         nc.scalar.activation(q_grouped[:], q_raw[:].rearrange("p t q -> p q t"), COPY)
-        vs_cols = tile_at(AT_K + 4096, [P, 4], F32, "vs_cols")
-        nc.scalar.copy(vs_cols[:], vs_bank[:, :, LAST])
         bias = tile_at(AT_K + 2048, [P, 4, P], F32, "bias")
         nc.scalar.activation(bias[:], spread[:].rearrange("p (i t) -> p t i", t=4), COPY, scale=slope_col[:])
         q_codes, q_scales = planes("q", NQ)
         nc.vector.quantize_mx(out=q_codes[:].bitcast(FP8X4), scales=q_scales[:], in_=q_grouped[:].rearrange("p q t -> p (q t)"))
         k_codes, k_scales = tile([P, N], U32, "k_codes"), tile_at(AT_Q, [P, N], U8, "k_scales")
-        k_flat = k_words[:].rearrange("p n u -> p (n u)").bitcast(BF16)
+        k_flat = shared[:, K0 : K0 + 2 * N].bitcast(BF16)
         scores = []
         for h in range(2):
             cols = slice(h * H, (h + 1) * H)
@@ -132,6 +132,10 @@ def tile_attend_ring_alibi_kernel(tc, qT, kT, vT, vs, pos, slope, offs, out):
             bank = psum.tile([P, H], F32, name=f"scores{h}", tag=f"scores{h}")
             nc.tensor.matmul_mx(out=bank[:], lhsT=q_codes[:].bitcast(FP8X4), lhsT_scale=q_scales[:], rhs=k_codes[:, cols].bitcast(FP8X4), rhs_scale=k_scales[:, cols], start=True, stop=True)
             scores.append(bank)
+        gather_scales(1)
+        vs_bank = psum.tile([P, 4, P], F32, name="vs_bank", tag="vs_bank")
+        for t in range(4):
+            nc.tensor.transpose(vs_bank[:, t, :], vs_dealt[:, t, :].bitcast(F32), ident[:])
 
         v_round = tile_at(AT_Q + 512, [P, T], BF16, "v_round")
         for h in range(2):
@@ -156,6 +160,9 @@ def tile_attend_ring_alibi_kernel(tc, qT, kT, vT, vs, pos, slope, offs, out):
                 nc.tensor.transpose(p_bank[:, 2 * u + e, :], pu[:, e, :], ident[:])
             sums.append(su)
 
+        vs_cols = tile_at(AT_V, [P, 4], F32, "vs_cols")
+        nc.scalar.copy(vs_cols[:], vs_bank[:, :, LAST])
+
         v_codes, v_scales = planes("v", DV)
 
         def turn_values(j, halves, grouped):
@@ -166,7 +173,7 @@ def tile_attend_ring_alibi_kernel(tc, qT, kT, vT, vs, pos, slope, offs, out):
             nc.scalar.copy(words, bank[:].rearrange("p u e -> p e u"))
             return grouped
 
-        v_grouped0 = turn_values(0, [v_listed0[:].bitcast(F32)[:, u : N // 2 : 2] for u in range(2)], tile_at(AT_V, [P, P, 4], BF16, "v_grouped0"))
+        v_grouped0 = turn_values(0, [v_listed0[:].bitcast(F32)[:, u : N // 2 : 2] for u in range(2)], tile_at(AT_V + 64, [P, P, 4], BF16, "v_grouped0"))
         total = tile([P, 1], F32, "total")
         nc.scalar.activation(total[:], sums[0][:], IDENTITY, bias=sums[1][:])
         v_listed1 = tile_at(AT_K + 2048, [P, N], BF16, "v_listed1")

@@ -35,31 +35,29 @@ def tile_attend_ring_alibi_kernel(tc, qT, kT, vT, vs, pos, slope, offs, out):
         def tile_at(offset, shape, dtype, name):
             return reuse.tile(shape, dtype, name=name, align_bytes=64, offset=offset)
 
-        AT_K, AT_Q, AT_V = 0, 8192, 11264
+        AT_B, AT_Q, AT_V, AT_R, AT_G = 0, 2048, 5120, 9216, 17408
         offsets = held.tile([P, N // 16], U16, name="offsets")
-        k_raw = [tile([P, 2, T], F32, "k_raw0"), tile_at(AT_K, [P, 2, T], F32, "k_raw1")]
+        k_raw = [tile([P, T], F32, f"k_raw{t}") for t in range(4)]
         v_raw = [tile_at(AT_V, [P, T], F32, "v_raw0"), tile([P, T], F32, "v_raw1")]
         q_raw = tile_at(AT_Q, [P, 4, NQ], F32, "q_raw")
-        pos_pool = tile([P, T], F32, "pos_pool")
-        vs_pool = tile([P, T], F32, "vs_pool")
+        pos_pool = tile_at(AT_R, [P, T], F32, "pos_pool")
+        vs_pool = tile_at(AT_R + 4096, [P, T], F32, "vs_pool")
         slope_rows = tile([P, P], F32, "slope_rows")
 
         k_rows = kT.rearrange("(p t) n -> p t n", t=4)
 
-        def load_keys(u, a, b):
-            nc.sync.dma_start(out=k_raw[u][:, :, a:b], in_=k_rows[:, 2 * u : 2 * u + 2, a:b])
-
+        ident = tile([P, P], F32, "ident")
+        make_identity(nc, ident[:])
         nc.vector.memset(pos_pool[0:LAST, :], 0.0)
         nc.gpsimd.memset(vs_pool[0:LAST, :], 0.0)
         nc.gpsimd.memset(slope_rows[0:LAST, :], 0.0)
         nc.sync.dma_start(offsets[:], offs)
-        load_keys(0, 0, 512)
-        nc.scalar.dma_start(out=pos_pool[LAST:P, :], in_=pos[0:1, :])
-        nc.scalar.dma_start(out=vs_pool[LAST:P, :], in_=vs[0:1, :])
-        nc.scalar.dma_start(out=slope_rows[LAST:P, :], in_=slope[0].rearrange("q o -> o q"))
-        load_keys(0, 512, T)
-        load_keys(1, 0, 512)
-        load_keys(1, 512, T)
+        nc.scalar.dma_start(out=k_raw[0][:], in_=k_rows[:, 0, :])
+        nc.sync.dma_start(out=pos_pool[LAST:P, :], in_=pos[0:1, :])
+        nc.sync.dma_start(out=vs_pool[LAST:P, :], in_=vs[0:1, :])
+        nc.sync.dma_start(out=slope_rows[LAST:P, :], in_=slope[0].rearrange("q o -> o q"))
+        for t in range(1, 4):
+            nc.sync.dma_start(out=k_raw[t][:], in_=k_rows[:, t, :])
         nc.sync.dma_start(out=q_raw[:], in_=qT[0].rearrange("(p t) q -> p t q", t=4))
         for h in range(2):
             nc.sync.dma_start(out=v_raw[0][:, h * 512 : (h + 1) * 512], in_=vT[0:P, h * 512 : (h + 1) * 512])
@@ -69,73 +67,63 @@ def tile_attend_ring_alibi_kernel(tc, qT, kT, vT, vs, pos, slope, offs, out):
         warm_out = tile([P, 1], F32, "warm_out")
         nc.vector.memset(warm[:], 0.0)
         nc.scalar.activation(warm_out[:], warm[:], EXP)
-        ident = tile([P, P], F32, "ident")
-        make_identity(nc, ident[:])
 
-        def pair_up(engine, pairs, raw, a, b):
-            dst = pairs[:, 2 * a : 2 * b].rearrange("p (n t) -> p n t", t=2)
-            src = raw[:, :, a:b].rearrange("p t n -> p n t")
+        def planes(name, width):
+            return tile([P, width], U32, name + "_codes"), tile([P, width], U8, name + "_scales")
+
+        def weave(engine, grouped, flat, a, b):
+            dst = grouped[:, 4 * a : 4 * b].rearrange("p (c i t) -> p c t i", i=4, t=4)
+            src = flat.rearrange("p (t c i) -> p c t i", t=4, i=4)[:, a // 4 : b // 4, :, :]
             if engine == "scalar":
                 nc.scalar.activation(dst, src, COPY)
             else:
                 nc.vector.tensor_copy(out=dst, in_=src)
 
-        def planes(name, width):
-            return tile([P, width], U32, name + "_codes"), tile([P, width], U8, name + "_scales")
-
-        K0 = N - 64
-        shared = tile([P, K0 + 2 * N], U32, "shared")
-        k_words = shared[:, K0 : K0 + 2 * N].rearrange("p (n u) -> p n u", u=2)
-        vs_dealt = shared[:, 0:N].rearrange("p (t s) -> p t s", t=4)
-
-        def gather_scales(h):
-            nc.vector.tensor_copy(vs_dealt[:, :, h * 64 : (h + 1) * 64].rearrange("p t s -> p s t"), vs_pool[:].bitcast(U32).indirect(offsets[:, h * 16 : (h + 1) * 16]))
-
         pos_listed = tile([P, N], F32, "pos_listed")
         nc.vector.tensor_copy(pos_listed[:], pos_pool[:].indirect(offsets[:]))
-        gather_scales(0)
-        k_pairs0 = tile([P, 2 * T], BF16, "k_pairs0")
-        pair_up("scalar", k_pairs0, k_raw[0], 0, 512)
+        vs_dealt = tile([P, 4, P], U32, "vs_dealt")
+        nc.vector.tensor_copy(vs_dealt[:].rearrange("p t s -> p s t"), vs_pool[:].bitcast(U32).indirect(offsets[:]))
         pos_bank = psum.tile([P, 4, P], F32, name="pos_bank", tag="p0")
         for j in range(4):
             nc.tensor.transpose(pos_bank[:, j, :], pos_listed[:, j * P : (j + 1) * P], ident[:])
         pos_cols = tile([P, 4], F32, "pos_cols")
         nc.scalar.copy(pos_cols[:], pos_bank[:, :, LAST])
+        vs_bank = psum.tile([P, 4, P], F32, name="vs_bank", tag="y0")
+        for t in range(4):
+            nc.tensor.transpose(vs_bank[:, t, :], vs_dealt[:, t, :].bitcast(F32), ident[:])
+        vs_cols = tile([P, 4], F32, "vs_cols")
+        nc.scalar.copy(vs_cols[:], vs_bank[:, :, LAST])
         spread = psum.tile([P, N], F32, name="spread", tag="y0")
         for j in range(4):
             nc.tensor.transpose(spread[:, j * P : (j + 1) * P], pos_cols[:, j : j + 1].to_broadcast([P, P]), ident[:])
         slope_bank = psum.tile([P, P], F32, name="slope_bank", tag="v_bank")
         nc.tensor.transpose(slope_bank[:], slope_rows[:], ident[:])
+        slope_col = tile_at(AT_G + 4096 - 64, [P, 32], F32, "slope_col")[:, 0:1]
+        nc.scalar.copy(slope_col, slope_bank[:, LAST:P])
+        bias = tile_at(AT_B, [P, 4, P], F32, "bias")
+        nc.scalar.activation(bias[:], spread[:].rearrange("p (i t) -> p t i", t=4), COPY, scale=slope_col)
 
-        pair_up("scalar", k_pairs0, k_raw[0], 512, 704)
-        pair_up("vector", k_pairs0, k_raw[0], 704, T)
-        nc.vector.tensor_copy(k_words[:, :, 0], k_pairs0[:].bitcast(U32).indirect(offsets[:]))
-        k_pairs1 = tile([P, 2 * T], BF16, "k_pairs1", "pos_listed")
-        pair_up("scalar", k_pairs1, k_raw[1], 0, 512)
-        pair_up("scalar", k_pairs1, k_raw[1], 512, 704)
-        pair_up("vector", k_pairs1, k_raw[1], 704, T)
-        nc.vector.tensor_copy(k_words[:, :, 1], k_pairs1[:].bitcast(U32).indirect(offsets[:]))
-        slope_col = tile_at(AT_K, [P, 1], F32, "slope_col")
-        nc.scalar.copy(slope_col[:], slope_bank[:, LAST:P])
-        q_grouped = tile_at(AT_K + 64, [P, NQ, 4], BF16, "q_grouped")
-        nc.scalar.activation(q_grouped[:], q_raw[:].rearrange("p t q -> p q t"), COPY)
-        bias = tile_at(AT_K + 2048, [P, 4, P], F32, "bias")
-        nc.scalar.activation(bias[:], spread[:].rearrange("p (i t) -> p t i", t=4), COPY, scale=slope_col[:])
+        k_listed = tile_at(AT_R + 2048, [P, 4 * N], BF16, "k_listed")
+        for t in range(3):
+            nc.vector.tensor_copy(k_listed[:, t * N : (t + 1) * N], k_raw[t][:].indirect(offsets[:]))
+        for h in range(2):
+            nc.vector.tensor_copy(k_listed[:, 3 * N + h * H : 3 * N + (h + 1) * H], k_raw[3][:].indirect(offsets[:, h * 16 : (h + 1) * 16]))
+        q_grouped = tile_at(AT_G + 4096, [P, 4 * NQ], BF16, "q_grouped")
+        weave("scalar", q_grouped, q_raw[:].rearrange("p t q -> p (t q)"), 0, NQ)
+        k_grouped = tile_at(AT_G, [P, 4 * N], BF16, "k_grouped")
+        weave("vector", k_grouped, k_listed[:], 0, H)
+        weave("vector", k_grouped, k_listed[:], H, 384)
+        weave("scalar", k_grouped, k_listed[:], 384, N)
         q_codes, q_scales = planes("q", NQ)
-        nc.vector.quantize_mx(out=q_codes[:].bitcast(FP8X4), scales=q_scales[:], in_=q_grouped[:].rearrange("p q t -> p (q t)"))
-        k_codes, k_scales = tile([P, N], U32, "k_codes"), tile_at(AT_Q, [P, N], U8, "k_scales")
-        k_flat = shared[:, K0 : K0 + 2 * N].bitcast(BF16)
+        nc.vector.quantize_mx(out=q_codes[:].bitcast(FP8X4), scales=q_scales[:], in_=q_grouped[:])
+        k_codes, k_scales = planes("k", N)
         scores = []
         for h in range(2):
             cols = slice(h * H, (h + 1) * H)
-            nc.vector.quantize_mx(out=k_codes[:, cols].bitcast(FP8X4), scales=k_scales[:, cols], in_=k_flat[:, 4 * h * H : 4 * (h + 1) * H])
+            nc.vector.quantize_mx(out=k_codes[:, cols].bitcast(FP8X4), scales=k_scales[:, cols], in_=k_grouped[:, 4 * h * H : 4 * (h + 1) * H])
             bank = psum.tile([P, H], F32, name=f"scores{h}", tag=f"scores{h}")
             nc.tensor.matmul_mx(out=bank[:], lhsT=q_codes[:].bitcast(FP8X4), lhsT_scale=q_scales[:], rhs=k_codes[:, cols].bitcast(FP8X4), rhs_scale=k_scales[:, cols], start=True, stop=True)
             scores.append(bank)
-        gather_scales(1)
-        vs_bank = psum.tile([P, 4, P], F32, name="vs_bank", tag="vs_bank")
-        for t in range(4):
-            nc.tensor.transpose(vs_bank[:, t, :], vs_dealt[:, t, :].bitcast(F32), ident[:])
 
         v_round = tile_at(AT_Q + 512, [P, T], BF16, "v_round")
         for h in range(2):
@@ -160,9 +148,6 @@ def tile_attend_ring_alibi_kernel(tc, qT, kT, vT, vs, pos, slope, offs, out):
                 nc.tensor.transpose(p_bank[:, 2 * u + e, :], pu[:, e, :], ident[:])
             sums.append(su)
 
-        vs_cols = tile_at(AT_V, [P, 4], F32, "vs_cols")
-        nc.scalar.copy(vs_cols[:], vs_bank[:, :, LAST])
-
         v_codes, v_scales = planes("v", DV)
 
         def turn_values(j, halves, grouped):
@@ -176,7 +161,7 @@ def tile_attend_ring_alibi_kernel(tc, qT, kT, vT, vs, pos, slope, offs, out):
         v_grouped0 = turn_values(0, [v_listed0[:].bitcast(F32)[:, u : N // 2 : 2] for u in range(2)], tile_at(AT_V + 64, [P, P, 4], BF16, "v_grouped0"))
         total = tile([P, 1], F32, "total")
         nc.scalar.activation(total[:], sums[0][:], IDENTITY, bias=sums[1][:])
-        v_listed1 = tile_at(AT_K + 2048, [P, N], BF16, "v_listed1")
+        v_listed1 = tile_at(AT_B, [P, N], BF16, "v_listed1")
         nc.vector.tensor_copy(v_listed1[:], v_raw[1][:].indirect(offsets[:]))
 
         w_grouped = tile([P, NQ, 4], BF16, "w_grouped")

@@ -7,6 +7,8 @@ NQ, D, N, T, DV = 128, 512, 512, 1024, 256
 P = 128
 LAST = P - 1
 H = N // 2
+SINKS = 64
+HEAD = 256
 FLOPS = 2 * NQ * N * (D + DV)
 
 F32 = mybir.dt.float32
@@ -35,7 +37,7 @@ def tile_attend_ring_alibi_kernel(tc, qT, kT, vT, vs, pos, slope, offs, out):
         def tile_at(offset, shape, dtype, name):
             return reuse.tile(shape, dtype, name=name, align_bytes=64, offset=offset)
 
-        AT_B, AT_Q, AT_V, AT_R, AT_G = 0, 2048, 5120, 9216, 17408
+        AT_B, AT_Q, AT_V, AT_R, AT_G, AT_S = 0, 2048, 5120, 9216, 17408, 22528
         offsets = held.tile([P, N // 16], U16, name="offsets")
         k_raw = [tile([P, T], F32, f"k_raw{t}") for t in range(4)]
         v_raw = [tile_at(AT_V, [P, T], F32, "v_raw0"), tile([P, T], F32, "v_raw1")]
@@ -49,15 +51,17 @@ def tile_attend_ring_alibi_kernel(tc, qT, kT, vT, vs, pos, slope, offs, out):
         ident = tile([P, P], F32, "ident")
         make_identity(nc, ident[:])
         nc.vector.memset(pos_pool[0:LAST, :], 0.0)
-        nc.gpsimd.memset(vs_pool[0:LAST, :], 0.0)
+        nc.vector.memset(vs_pool[0:LAST, :], 0.0)
         nc.gpsimd.memset(slope_rows[0:LAST, :], 0.0)
         nc.sync.dma_start(offsets[:], offs)
         nc.scalar.dma_start(out=k_raw[0][:], in_=k_rows[:, 0, :])
         nc.sync.dma_start(out=pos_pool[LAST:P, :], in_=pos[0:1, :])
         nc.sync.dma_start(out=vs_pool[LAST:P, :], in_=vs[0:1, :])
         nc.sync.dma_start(out=slope_rows[LAST:P, :], in_=slope[0].rearrange("q o -> o q"))
-        for t in range(1, 4):
-            nc.sync.dma_start(out=k_raw[t][:], in_=k_rows[:, t, :])
+        nc.sync.dma_start(out=k_raw[1][:], in_=k_rows[:, 1, :])
+        nc.sync.dma_start(out=k_raw[3][:, 0:HEAD], in_=k_rows[:, 3, 0:HEAD])
+        nc.sync.dma_start(out=k_raw[2][:], in_=k_rows[:, 2, :])
+        nc.sync.dma_start(out=k_raw[3][:, HEAD:T], in_=k_rows[:, 3, HEAD:T])
         nc.sync.dma_start(out=q_raw[:], in_=qT[0].rearrange("(p t) q -> p t q", t=4))
         for h in range(2):
             nc.sync.dma_start(out=v_raw[0][:, h * 512 : (h + 1) * 512], in_=vT[0:P, h * 512 : (h + 1) * 512])
@@ -103,25 +107,32 @@ def tile_attend_ring_alibi_kernel(tc, qT, kT, vT, vs, pos, slope, offs, out):
         bias = tile_at(AT_B, [P, 4, P], F32, "bias")
         nc.scalar.activation(bias[:], spread[:].rearrange("p (i t) -> p t i", t=4), COPY, scale=slope_col)
 
-        k_listed = tile_at(AT_R + 2048, [P, 4 * N], BF16, "k_listed")
-        for t in range(3):
-            nc.vector.tensor_copy(k_listed[:, t * N : (t + 1) * N], k_raw[t][:].indirect(offsets[:]))
-        for h in range(2):
-            nc.vector.tensor_copy(k_listed[:, 3 * N + h * H : 3 * N + (h + 1) * H], k_raw[3][:].indirect(offsets[:, h * 16 : (h + 1) * 16]))
+        k_listed = tile_at(AT_R, [P, 4 * N], F32, "k_listed")
+
+        def gather_keys(t, a, b, tokens):
+            nc.vector.tensor_copy(k_listed[:, t * N + a : t * N + b], k_raw[t][:, 0:tokens].indirect(offsets[:, a // 16 : b // 16]))
+
+        gather_keys(0, 0, N, T)
+        gather_keys(1, 0, N, T)
+        gather_keys(3, 0, SINKS, HEAD)
+        gather_keys(2, 0, N, T)
+        gather_keys(3, SINKS, H, T)
+        gather_keys(3, H, N, T)
+        k_grouped = tile_at(AT_G, [P, 4 * N], BF16, "k_grouped")
+        weave("scalar", k_grouped, k_listed[:], 0, SINKS)
         q_grouped = tile_at(AT_G + 4096, [P, 4 * NQ], BF16, "q_grouped")
         weave("scalar", q_grouped, q_raw[:].rearrange("p t q -> p (t q)"), 0, NQ)
-        k_grouped = tile_at(AT_G, [P, 4 * N], BF16, "k_grouped")
-        weave("vector", k_grouped, k_listed[:], 0, H)
-        weave("vector", k_grouped, k_listed[:], H, 384)
-        weave("scalar", k_grouped, k_listed[:], 384, N)
+        weave("vector", k_grouped, k_listed[:], SINKS, H)
+        weave("vector", k_grouped, k_listed[:], H, 416)
+        weave("scalar", k_grouped, k_listed[:], 416, N)
         q_codes, q_scales = planes("q", NQ)
         nc.vector.quantize_mx(out=q_codes[:].bitcast(FP8X4), scales=q_scales[:], in_=q_grouped[:])
         k_codes, k_scales = planes("k", N)
         scores = []
-        for h in range(2):
-            cols = slice(h * H, (h + 1) * H)
-            nc.vector.quantize_mx(out=k_codes[:, cols].bitcast(FP8X4), scales=k_scales[:, cols], in_=k_grouped[:, 4 * h * H : 4 * (h + 1) * H])
-            bank = psum.tile([P, H], F32, name=f"scores{h}", tag=f"scores{h}")
+        for j in range(4):
+            cols = slice(j * P, (j + 1) * P)
+            nc.vector.quantize_mx(out=k_codes[:, cols].bitcast(FP8X4), scales=k_scales[:, cols], in_=k_grouped[:, 4 * j * P : 4 * (j + 1) * P])
+            bank = psum.tile([P, P], F32, name=f"scores{j}", tag=f"scores{j}")
             nc.tensor.matmul_mx(out=bank[:], lhsT=q_codes[:].bitcast(FP8X4), lhsT_scale=q_scales[:], rhs=k_codes[:, cols].bitcast(FP8X4), rhs_scale=k_scales[:, cols], start=True, stop=True)
             scores.append(bank)
 
@@ -131,22 +142,19 @@ def tile_attend_ring_alibi_kernel(tc, qT, kT, vT, vs, pos, slope, offs, out):
         v_listed0 = tile([P, N], BF16, "v_listed0")
         nc.scalar.activation(v_listed0[:], v_round[:].indirect(offsets[:]), COPY)
 
-        s = tile([P, 4, P], F32, "s")
-        for h in range(2):
-            part = slice(h * 64, (h + 1) * 64)
-            nc.vector.tensor_tensor(s[:, :, part], scores[h][:].rearrange("p (i t) -> p t i", t=4), bias[:, :, part], ADD)
+        s = tile_at(AT_S, [P, 4, P], F32, "s")
+        for j in range(4):
+            part = slice(j * 32, (j + 1) * 32)
+            nc.vector.tensor_tensor(s[:, :, part], scores[j][:].rearrange("p (i t) -> p t i", t=4), bias[:, :, part], ADD)
         minus_m = tile([P, 1], F32, "minus_m")
         nc.vector.tensor_reduce(out=minus_m[:], in_=s[:].rearrange("p t i -> p (t i)"), axis=X, op=MAX, negate=True)
 
         p_bank = psum.tile([P, 4, P], F32, name="p_bank", tag="p0")
-        sums = []
-        for u in range(2):
-            pu = tile_at(AT_V, [P, 2, P], F32, "p0") if u == 0 else tile([P, 2, P], F32, "p1")
-            su = tile([P, 1], F32, f"sum{u}")
-            nc.scalar.activation(pu[:], s[:, 2 * u : 2 * u + 2, :], EXP, bias=minus_m[:], accum_out=su[:])
-            for e in range(2):
-                nc.tensor.transpose(p_bank[:, 2 * u + e, :], pu[:, e, :], ident[:])
-            sums.append(su)
+        sums = tile([P, 4], F32, "sums")
+        p = tile_at(AT_V, [P, 4 * P], F32, "p")
+        for t in range(4):
+            nc.scalar.activation(p[:, t * P : (t + 1) * P], s[:, t, :], EXP, bias=minus_m[:], accum_out=sums[:, t : t + 1])
+            nc.tensor.transpose(p_bank[:, t, :], p[:, t * P : (t + 1) * P], ident[:])
 
         v_codes, v_scales = planes("v", DV)
 
@@ -158,9 +166,10 @@ def tile_attend_ring_alibi_kernel(tc, qT, kT, vT, vs, pos, slope, offs, out):
             nc.scalar.copy(words, bank[:].rearrange("p u e -> p e u"))
             return grouped
 
-        v_grouped0 = turn_values(0, [v_listed0[:].bitcast(F32)[:, u : N // 2 : 2] for u in range(2)], tile_at(AT_V + 64, [P, P, 4], BF16, "v_grouped0"))
+        v_grouped0 = turn_values(0, [v_listed0[:].bitcast(F32)[:, u : N // 2 : 2] for u in range(2)], tile_at(AT_S, [P, P, 4], BF16, "v_grouped0"))
         total = tile([P, 1], F32, "total")
-        nc.scalar.activation(total[:], sums[0][:], IDENTITY, bias=sums[1][:])
+        sums_again = tile([P, 4], F32, "sums_again")
+        nc.scalar.activation(sums_again[:], sums[:], COPY, accum_out=total[:])
         v_listed1 = tile_at(AT_B, [P, N], BF16, "v_listed1")
         nc.vector.tensor_copy(v_listed1[:], v_raw[1][:].indirect(offsets[:]))
 

@@ -92,11 +92,9 @@ def tile_attend_ring_alibi_kernel(tc, qT, kT, vT, vs, pos, slope, offs, out):
             nc.tensor.transpose(pos_bank[:, j, :], pos_listed[:, j * P : (j + 1) * P], ident[:])
         pos_cols = tile([P, 4], F32, "pos_cols")
         nc.scalar.copy(pos_cols[:], pos_bank[:, :, LAST])
-        vs_bank = psum.tile([P, 4, P], F32, name="vs_bank", tag="y0")
+        vs_bank = psum.tile([P, 4, P], F32, name="vs_bank", tag="vs_bank")
         for t in range(4):
             nc.tensor.transpose(vs_bank[:, t, :], vs_dealt[:, t, :].bitcast(F32), ident[:])
-        vs_cols = tile([P, 4], F32, "vs_cols")
-        nc.scalar.copy(vs_cols[:], vs_bank[:, :, LAST])
         spread = psum.tile([P, N], F32, name="spread", tag="y0")
         for j in range(4):
             nc.tensor.transpose(spread[:, j * P : (j + 1) * P], pos_cols[:, j : j + 1].to_broadcast([P, P]), ident[:])
@@ -126,12 +124,13 @@ def tile_attend_ring_alibi_kernel(tc, qT, kT, vT, vs, pos, slope, offs, out):
         weave("vector", k_grouped, k_listed[:], H, 416)
         weave("scalar", k_grouped, k_listed[:], 416, N)
         q_codes, q_scales = planes("q", NQ)
-        nc.vector.quantize_mx(out=q_codes[:].bitcast(FP8X4), scales=q_scales[:], in_=q_grouped[:])
         k_codes, k_scales = planes("k", N)
         scores = []
         for j in range(4):
             cols = slice(j * P, (j + 1) * P)
             nc.vector.quantize_mx(out=k_codes[:, cols].bitcast(FP8X4), scales=k_scales[:, cols], in_=k_grouped[:, 4 * j * P : 4 * (j + 1) * P])
+            if j == 0:
+                nc.vector.quantize_mx(out=q_codes[:].bitcast(FP8X4), scales=q_scales[:], in_=q_grouped[:])
             bank = psum.tile([P, P], F32, name=f"scores{j}", tag=f"scores{j}")
             nc.tensor.matmul_mx(out=bank[:], lhsT=q_codes[:].bitcast(FP8X4), lhsT_scale=q_scales[:], rhs=k_codes[:, cols].bitcast(FP8X4), rhs_scale=k_scales[:, cols], start=True, stop=True)
             scores.append(bank)
@@ -155,28 +154,33 @@ def tile_attend_ring_alibi_kernel(tc, qT, kT, vT, vs, pos, slope, offs, out):
         for t in range(4):
             nc.scalar.activation(p[:, t * P : (t + 1) * P], s[:, t, :], EXP, bias=minus_m[:], accum_out=sums[:, t : t + 1])
             nc.tensor.transpose(p_bank[:, t, :], p[:, t * P : (t + 1) * P], ident[:])
+        vs_cols = tile_at(AT_S, [P, 4], F32, "vs_cols")
+        nc.scalar.copy(vs_cols[:], vs_bank[:, :, LAST])
 
         v_codes, v_scales = planes("v", DV)
 
         def turn_values(j, halves, grouped):
-            bank = psum.tile([P, 2, P], F32, name=f"v_bank{j}", tag="v_bank")
+            bank = psum.tile([P, 2, P], F32, name=f"v_bank{j}", tag="v_bank" if j == 0 else "vs_bank")
             for u in range(2):
                 nc.tensor.transpose(bank[:, u, :], halves[u], ident[:])
             words = grouped[:].rearrange("p e t -> p (e t)").bitcast(F32).rearrange("p (e u) -> p e u", u=2)
-            nc.scalar.copy(words, bank[:].rearrange("p u e -> p e u"))
+            if j == 0:
+                nc.vector.tensor_copy(words, bank[:].rearrange("p u e -> p e u"))
+            else:
+                nc.scalar.copy(words, bank[:].rearrange("p u e -> p e u"))
             return grouped
 
-        v_grouped0 = turn_values(0, [v_listed0[:].bitcast(F32)[:, u : N // 2 : 2] for u in range(2)], tile_at(AT_S, [P, P, 4], BF16, "v_grouped0"))
+        v_grouped0 = turn_values(0, [v_listed0[:].bitcast(F32)[:, u : N // 2 : 2] for u in range(2)], tile_at(AT_B + 1024, [P, P, 4], BF16, "v_grouped0"))
         total = tile([P, 1], F32, "total")
         sums_again = tile([P, 4], F32, "sums_again")
         nc.scalar.activation(sums_again[:], sums[:], COPY, accum_out=total[:])
         v_listed1 = tile_at(AT_B, [P, N], BF16, "v_listed1")
-        nc.vector.tensor_copy(v_listed1[:], v_raw[1][:].indirect(offsets[:]))
+        nc.vector.tensor_copy(v_listed1[:].rearrange("p (u s e) -> p s u e", u=2, e=2), v_raw[1][:].indirect(offsets[:]))
+        nc.vector.quantize_mx(out=v_codes[:, 0:128].bitcast(FP8X4), scales=v_scales[:, 0:128], in_=v_grouped0[:].rearrange("p e t -> p (e t)"))
 
         w_grouped = tile([P, NQ, 4], BF16, "w_grouped")
         nc.vector.tensor_tensor(w_grouped[:], p_bank[:].rearrange("p t q -> p q t"), vs_cols[:].unsqueeze(1).to_broadcast([P, NQ, 4]), MULT)
-        v_grouped1 = turn_values(1, [v_listed1[:].bitcast(F32)[:, u : N // 2 : 2] for u in range(2)], tile([P, P, 4], BF16, "v_grouped1"))
-        nc.vector.quantize_mx(out=v_codes[:, 0:128].bitcast(FP8X4), scales=v_scales[:, 0:128], in_=v_grouped0[:].rearrange("p e t -> p (e t)"))
+        v_grouped1 = turn_values(1, [v_listed1[:].bitcast(F32)[:, u * P : (u + 1) * P] for u in range(2)], tile([P, P, 4], BF16, "v_grouped1"))
         w_codes, w_scales = planes("w", NQ)
         nc.vector.quantize_mx(out=w_codes[:].bitcast(FP8X4), scales=w_scales[:], in_=w_grouped[:].rearrange("p q t -> p (q t)"))
         nc.vector.quantize_mx(out=v_codes[:, 128:256].bitcast(FP8X4), scales=v_scales[:, 128:256], in_=v_grouped1[:].rearrange("p e t -> p (e t)"))

@@ -87,19 +87,19 @@ def tile_attend_ring_alibi_kernel(tc, qT, kT, vT, vs, pos, slope, offs, out):
         nc.vector.tensor_copy(pos_listed[:], pos_pool[:].indirect(offsets[:]))
         vs_dealt = tile([P, 4, P], U32, "vs_dealt")
         nc.vector.tensor_copy(vs_dealt[:].rearrange("p t s -> p s t"), vs_pool[:].bitcast(U32).indirect(offsets[:]))
-        pos_bank = psum.tile([P, 4, P], F32, name="pos_bank", tag="p0")
+        pos_bank = psum.tile([P, 4, P], F32, name="pos_bank", tag="vs_bank")
         for j in range(4):
             nc.tensor.transpose(pos_bank[:, j, :], pos_listed[:, j * P : (j + 1) * P], ident[:])
         pos_cols = tile([P, 4], F32, "pos_cols")
         nc.scalar.copy(pos_cols[:], pos_bank[:, :, LAST])
-        vs_bank = psum.tile([P, 4, P], F32, name="vs_bank", tag="vs_bank")
-        for t in range(4):
-            nc.tensor.transpose(vs_bank[:, t, :], vs_dealt[:, t, :].bitcast(F32), ident[:])
+        slope_bank = psum.tile([P, P], F32, name="slope_bank", tag="v_bank")
+        nc.tensor.transpose(slope_bank[:], slope_rows[:], ident[:])
         spread = psum.tile([P, N], F32, name="spread", tag="y0")
         for j in range(4):
             nc.tensor.transpose(spread[:, j * P : (j + 1) * P], pos_cols[:, j : j + 1].to_broadcast([P, P]), ident[:])
-        slope_bank = psum.tile([P, P], F32, name="slope_bank", tag="v_bank")
-        nc.tensor.transpose(slope_bank[:], slope_rows[:], ident[:])
+        vs_bank = psum.tile([P, 4, P], F32, name="vs_bank", tag="vs_bank")
+        for t in range(4):
+            nc.tensor.transpose(vs_bank[:, t, :], vs_dealt[:, t, :].bitcast(F32), ident[:])
         slope_col = tile_at(AT_G + 4096 - 64, [P, 32], F32, "slope_col")[:, 0:1]
         nc.scalar.copy(slope_col, slope_bank[:, LAST:P])
         bias = tile_at(AT_B, [P, 4, P], F32, "bias")
@@ -124,15 +124,16 @@ def tile_attend_ring_alibi_kernel(tc, qT, kT, vT, vs, pos, slope, offs, out):
         weave("vector", k_grouped, k_listed[:], H, 416)
         weave("scalar", k_grouped, k_listed[:], 416, N)
         q_codes, q_scales = planes("q", NQ)
-        k_codes, k_scales = planes("k", N)
+        k_codes = tile([P, N], U32, "k_codes")
+        k_scales = [tile([P, P], U8, f"k_scales{j}") if j < 2 else tile_at(AT_G + 4096 + j * P, [P, P], U8, f"k_scales{j}") for j in range(4)]
         scores = []
         for j in range(4):
             cols = slice(j * P, (j + 1) * P)
-            nc.vector.quantize_mx(out=k_codes[:, cols].bitcast(FP8X4), scales=k_scales[:, cols], in_=k_grouped[:, 4 * j * P : 4 * (j + 1) * P])
+            nc.vector.quantize_mx(out=k_codes[:, cols].bitcast(FP8X4), scales=k_scales[j][:], in_=k_grouped[:, 4 * j * P : 4 * (j + 1) * P])
             if j == 0:
                 nc.vector.quantize_mx(out=q_codes[:].bitcast(FP8X4), scales=q_scales[:], in_=q_grouped[:])
             bank = psum.tile([P, P], F32, name=f"scores{j}", tag=f"scores{j}")
-            nc.tensor.matmul_mx(out=bank[:], lhsT=q_codes[:].bitcast(FP8X4), lhsT_scale=q_scales[:], rhs=k_codes[:, cols].bitcast(FP8X4), rhs_scale=k_scales[:, cols], start=True, stop=True)
+            nc.tensor.matmul_mx(out=bank[:], lhsT=q_codes[:].bitcast(FP8X4), lhsT_scale=q_scales[:], rhs=k_codes[:, cols].bitcast(FP8X4), rhs_scale=k_scales[j][:], start=True, stop=True)
             scores.append(bank)
 
         v_round = tile_at(AT_Q + 512, [P, T], BF16, "v_round")
@@ -170,12 +171,12 @@ def tile_attend_ring_alibi_kernel(tc, qT, kT, vT, vs, pos, slope, offs, out):
                 nc.scalar.copy(words, bank[:].rearrange("p u e -> p e u"))
             return grouped
 
+        v_listed1 = tile_at(AT_B, [P, N], BF16, "v_listed1")
+        nc.vector.tensor_copy(v_listed1[:].rearrange("p (u s e) -> p s u e", u=2, e=2), v_raw[1][:].indirect(offsets[:]))
         v_grouped0 = turn_values(0, [v_listed0[:].bitcast(F32)[:, u : N // 2 : 2] for u in range(2)], tile_at(AT_B + 1024, [P, P, 4], BF16, "v_grouped0"))
         total = tile([P, 1], F32, "total")
         sums_again = tile([P, 4], F32, "sums_again")
         nc.scalar.activation(sums_again[:], sums[:], COPY, accum_out=total[:])
-        v_listed1 = tile_at(AT_B, [P, N], BF16, "v_listed1")
-        nc.vector.tensor_copy(v_listed1[:].rearrange("p (u s e) -> p s u e", u=2, e=2), v_raw[1][:].indirect(offsets[:]))
         nc.vector.quantize_mx(out=v_codes[:, 0:128].bitcast(FP8X4), scales=v_scales[:, 0:128], in_=v_grouped0[:].rearrange("p e t -> p (e t)"))
 
         w_grouped = tile([P, NQ, 4], BF16, "w_grouped")

@@ -37,7 +37,7 @@ def tile_attend_ring_alibi_kernel(tc, qT, kT, vT, vs, pos, slope, offs, out):
         def tile_at(offset, shape, dtype, name):
             return reuse.tile(shape, dtype, name=name, align_bytes=64, offset=offset)
 
-        AT_B, AT_Q, AT_V, AT_R, AT_G, AT_S = 0, 2048, 5120, 9216, 17408, 22528
+        AT_B, AT_Q, AT_V, AT_R, AT_G = 0, 2048, 5120, 9216, 17408
         offsets = held.tile([P, N // 16], U16, name="offsets")
         k_raw = [tile([P, T], F32, f"k_raw{t}") for t in range(4)]
         v_raw = [tile_at(AT_V, [P, T], F32, "v_raw0"), tile([P, T], F32, "v_raw1")]
@@ -76,7 +76,7 @@ def tile_attend_ring_alibi_kernel(tc, qT, kT, vT, vs, pos, slope, offs, out):
             return tile([P, width], U32, name + "_codes"), tile([P, width], U8, name + "_scales")
 
         def weave(engine, grouped, flat, a, b):
-            dst = grouped[:, 4 * a : 4 * b].rearrange("p (c i t) -> p c t i", i=4, t=4)
+            dst = grouped.rearrange("p (c i t) -> p c t i", i=4, t=4)
             src = flat.rearrange("p (t c i) -> p c t i", t=4, i=4)[:, a // 4 : b // 4, :, :]
             if engine == "scalar":
                 nc.scalar.activation(dst, src, COPY)
@@ -87,23 +87,26 @@ def tile_attend_ring_alibi_kernel(tc, qT, kT, vT, vs, pos, slope, offs, out):
         nc.vector.tensor_copy(pos_listed[:], pos_pool[:].indirect(offsets[:]))
         vs_dealt = tile([P, 4, P], U32, "vs_dealt")
         nc.vector.tensor_copy(vs_dealt[:].rearrange("p t s -> p s t"), vs_pool[:].bitcast(U32).indirect(offsets[:]))
-        pos_bank = psum.tile([P, 4, P], F32, name="pos_bank", tag="vs_bank")
-        for j in range(4):
-            nc.tensor.transpose(pos_bank[:, j, :], pos_listed[:, j * P : (j + 1) * P], ident[:])
-        pos_cols = tile([P, 4], F32, "pos_cols")
-        nc.scalar.copy(pos_cols[:], pos_bank[:, :, LAST])
+        pos_cols = []
+        for h in range(2):
+            pos_bank = psum.tile([P, 2, P], F32, name=f"pos_bank{h}", tag=("scores1", "vs_bank")[h])
+            for j in range(2):
+                nc.tensor.transpose(pos_bank[:, j, :], pos_listed[:, (2 * h + j) * P : (2 * h + j + 1) * P], ident[:])
+            pos_cols.append(tile([P, 2], F32, f"pos_cols{h}"))
+            nc.scalar.copy(pos_cols[h][:], pos_bank[:, :, LAST])
         slope_bank = psum.tile([P, P], F32, name="slope_bank", tag="v_bank")
         nc.tensor.transpose(slope_bank[:], slope_rows[:], ident[:])
-        spread = psum.tile([P, N], F32, name="spread", tag="y0")
-        for j in range(4):
-            nc.tensor.transpose(spread[:, j * P : (j + 1) * P], pos_cols[:, j : j + 1].to_broadcast([P, P]), ident[:])
-        vs_bank = psum.tile([P, 4, P], F32, name="vs_bank", tag="vs_bank")
-        for t in range(4):
-            nc.tensor.transpose(vs_bank[:, t, :], vs_dealt[:, t, :].bitcast(F32), ident[:])
         slope_col = tile_at(AT_G + 4096 - 64, [P, 32], F32, "slope_col")[:, 0:1]
         nc.scalar.copy(slope_col, slope_bank[:, LAST:P])
         bias = tile_at(AT_B, [P, 4, P], F32, "bias")
-        nc.scalar.activation(bias[:], spread[:].rearrange("p (i t) -> p t i", t=4), COPY, scale=slope_col)
+        for h in range(2):
+            spread = psum.tile([P, H], F32, name=f"spread{h}", tag=("scores2", "y0")[h])
+            for j in range(2):
+                nc.tensor.transpose(spread[:, j * P : (j + 1) * P], pos_cols[h][:, j : j + 1].to_broadcast([P, P]), ident[:])
+            nc.scalar.activation(bias[:, :, h * 64 : (h + 1) * 64], spread[:].rearrange("p (i t) -> p t i", t=4), COPY, scale=slope_col)
+        vs_bank = psum.tile([P, 4, P], F32, name="vs_bank", tag="vs_bank")
+        for t in range(4):
+            nc.tensor.transpose(vs_bank[:, t, :], vs_dealt[:, t, :].bitcast(F32), ident[:])
 
         k_listed = tile_at(AT_R, [P, 4 * N], F32, "k_listed")
 
@@ -116,33 +119,33 @@ def tile_attend_ring_alibi_kernel(tc, qT, kT, vT, vs, pos, slope, offs, out):
         gather_keys(2, 0, N, T)
         gather_keys(3, SINKS, H, T)
         gather_keys(3, H, N, T)
-        k_grouped = tile_at(AT_G, [P, 4 * N], BF16, "k_grouped")
-        weave("scalar", k_grouped, k_listed[:], 0, SINKS)
+        k_grouped = tile_at(AT_G + 1024, [P, 12 * P], BF16, "k_grouped")
+        weave("scalar", k_grouped[:, 0 : 4 * SINKS], k_listed[:], 0, SINKS)
         q_grouped = tile_at(AT_G + 4096, [P, 4 * NQ], BF16, "q_grouped")
-        weave("scalar", q_grouped, q_raw[:].rearrange("p t q -> p (t q)"), 0, NQ)
-        weave("vector", k_grouped, k_listed[:], SINKS, H)
-        weave("vector", k_grouped, k_listed[:], H, 416)
-        weave("scalar", k_grouped, k_listed[:], 416, N)
+        weave("scalar", q_grouped[:], q_raw[:].rearrange("p t q -> p (t q)"), 0, NQ)
+        k_tail = tile_at(AT_Q, [P, 4 * P], BF16, "k_tail")
+        weave("scalar", k_tail[:], k_listed[:], 3 * P, N)
+        weave("vector", k_grouped[:, 4 * SINKS : 4 * H], k_listed[:], SINKS, H)
+        weave("vector", k_grouped[:, 4 * H : 12 * P], k_listed[:], H, 3 * P)
         q_codes, q_scales = planes("q", NQ)
         k_codes = tile([P, N], U32, "k_codes")
-        k_scales = [tile([P, P], U8, f"k_scales{j}") if j < 2 else tile_at(AT_G + 4096 + j * P, [P, P], U8, f"k_scales{j}") for j in range(4)]
+        k_scales = tile_at(AT_Q + 1024, [P, N], U8, "k_scales")
+        nc.vector.quantize_mx(out=q_codes[:].bitcast(FP8X4), scales=q_scales[:], in_=q_grouped[:])
         scores = []
         for j in range(4):
             cols = slice(j * P, (j + 1) * P)
-            nc.vector.quantize_mx(out=k_codes[:, cols].bitcast(FP8X4), scales=k_scales[j][:], in_=k_grouped[:, 4 * j * P : 4 * (j + 1) * P])
-            if j == 0:
-                nc.vector.quantize_mx(out=q_codes[:].bitcast(FP8X4), scales=q_scales[:], in_=q_grouped[:])
+            nc.vector.quantize_mx(out=k_codes[:, cols].bitcast(FP8X4), scales=k_scales[:, cols], in_=k_grouped[:, 4 * j * P : 4 * (j + 1) * P] if j < 3 else k_tail[:])
             bank = psum.tile([P, P], F32, name=f"scores{j}", tag=f"scores{j}")
-            nc.tensor.matmul_mx(out=bank[:], lhsT=q_codes[:].bitcast(FP8X4), lhsT_scale=q_scales[:], rhs=k_codes[:, cols].bitcast(FP8X4), rhs_scale=k_scales[j][:], start=True, stop=True)
+            nc.tensor.matmul_mx(out=bank[:], lhsT=q_codes[:].bitcast(FP8X4), lhsT_scale=q_scales[:], rhs=k_codes[:, cols].bitcast(FP8X4), rhs_scale=k_scales[:, cols], start=True, stop=True)
             scores.append(bank)
 
-        v_round = tile_at(AT_Q + 512, [P, T], BF16, "v_round")
+        v_round = tile_at(AT_G + 4096 + 960, [P, T], BF16, "v_round")
         for h in range(2):
             nc.scalar.activation(v_round[:, h * 512 : (h + 1) * 512], v_raw[0][:, h * 512 : (h + 1) * 512], COPY)
         v_listed0 = tile([P, N], BF16, "v_listed0")
         nc.scalar.activation(v_listed0[:], v_round[:].indirect(offsets[:]), COPY)
 
-        s = tile_at(AT_S, [P, 4, P], F32, "s")
+        s = tile_at(AT_R, [P, 4, P], F32, "s")
         for j in range(4):
             part = slice(j * 32, (j + 1) * 32)
             nc.vector.tensor_tensor(s[:, :, part], scores[j][:].rearrange("p (i t) -> p t i", t=4), bias[:, :, part], ADD)
@@ -155,7 +158,7 @@ def tile_attend_ring_alibi_kernel(tc, qT, kT, vT, vs, pos, slope, offs, out):
         for t in range(4):
             nc.scalar.activation(p[:, t * P : (t + 1) * P], s[:, t, :], EXP, bias=minus_m[:], accum_out=sums[:, t : t + 1])
             nc.tensor.transpose(p_bank[:, t, :], p[:, t * P : (t + 1) * P], ident[:])
-        vs_cols = tile_at(AT_S, [P, 4], F32, "vs_cols")
+        vs_cols = tile_at(AT_R, [P, 4], F32, "vs_cols")
         nc.scalar.copy(vs_cols[:], vs_bank[:, :, LAST])
 
         v_codes, v_scales = planes("v", DV)

@@ -139,9 +139,9 @@ def tile_attend_ring_alibi_kernel(tc, qT, kT, vT, vs, pos, slope, offs, out):
             nc.tensor.matmul_mx(out=bank[:], lhsT=q_codes[:].bitcast(FP8X4), lhsT_scale=q_scales[:], rhs=k_codes[:, cols].bitcast(FP8X4), rhs_scale=k_scales[:, cols], start=True, stop=True)
             scores.append(bank)
 
-        v_round = tile_at(AT_G + 4096 + 960, [P, T], BF16, "v_round")
-        for h in range(2):
-            nc.scalar.activation(v_round[:, h * 512 : (h + 1) * 512], v_raw[0][:, h * 512 : (h + 1) * 512], COPY)
+        v_round = tile([P, T], BF16, "v_round")
+        for a, b in ((0, 256), (256, 512), (512, T)):
+            nc.scalar.activation(v_round[:, a:b], v_raw[0][:, a:b], COPY)
         v_listed0 = tile([P, N], BF16, "v_listed0")
         nc.scalar.activation(v_listed0[:], v_round[:].indirect(offsets[:]), COPY)
 

@@ -119,12 +119,11 @@ def tile_attend_ring_alibi_kernel(tc, qT, kT, vT, vs, pos, slope, offs, out):
         gather_keys(2, 0, N, T)
         gather_keys(3, SINKS, H, T)
         gather_keys(3, H, N, T)
-        k_grouped = tile_at(AT_G + 1024, [P, 12 * P], BF16, "k_grouped")
+        k_grouped = tile_at(AT_G, [P, 4 * N], BF16, "k_grouped")
         weave("scalar", k_grouped[:, 0 : 4 * SINKS], k_listed[:], 0, SINKS)
         q_grouped = tile_at(AT_G + 4096, [P, 4 * NQ], BF16, "q_grouped")
         weave("scalar", q_grouped[:], q_raw[:].rearrange("p t q -> p (t q)"), 0, NQ)
-        k_tail = tile_at(AT_Q, [P, 4 * P], BF16, "k_tail")
-        weave("scalar", k_tail[:], k_listed[:], 3 * P, N)
+        weave("scalar", k_grouped[:, 12 * P : 4 * N], k_listed[:], 3 * P, N)
         weave("vector", k_grouped[:, 4 * SINKS : 4 * H], k_listed[:], SINKS, H)
         weave("vector", k_grouped[:, 4 * H : 12 * P], k_listed[:], H, 3 * P)
         q_codes, q_scales = planes("q", NQ)
@@ -134,7 +133,7 @@ def tile_attend_ring_alibi_kernel(tc, qT, kT, vT, vs, pos, slope, offs, out):
         scores = []
         for j in range(4):
             cols = slice(j * P, (j + 1) * P)
-            nc.vector.quantize_mx(out=k_codes[:, cols].bitcast(FP8X4), scales=k_scales[:, cols], in_=k_grouped[:, 4 * j * P : 4 * (j + 1) * P] if j < 3 else k_tail[:])
+            nc.vector.quantize_mx(out=k_codes[:, cols].bitcast(FP8X4), scales=k_scales[:, cols], in_=k_grouped[:, 4 * j * P : 4 * (j + 1) * P])
             bank = psum.tile([P, P], F32, name=f"scores{j}", tag=f"scores{j}")
             nc.tensor.matmul_mx(out=bank[:], lhsT=q_codes[:].bitcast(FP8X4), lhsT_scale=q_scales[:], rhs=k_codes[:, cols].bitcast(FP8X4), rhs_scale=k_scales[:, cols], start=True, stop=True)
             scores.append(bank)

@@ -123,9 +123,9 @@ def tile_attend_ring_alibi_kernel(tc, qT, kT, vT, vs, pos, slope, offs, out):
         weave("scalar", k_grouped[:, 0 : 4 * SINKS], k_listed[:], 0, SINKS)
         q_grouped = tile_at(AT_G + 4096, [P, 4 * NQ], BF16, "q_grouped")
         weave("scalar", q_grouped[:], q_raw[:].rearrange("p t q -> p (t q)"), 0, NQ)
-        weave("scalar", k_grouped[:, 12 * P : 4 * N], k_listed[:], 3 * P, N)
+        weave("scalar", k_grouped[:, 4 * 416 : 4 * N], k_listed[:], 416, N)
         weave("vector", k_grouped[:, 4 * SINKS : 4 * H], k_listed[:], SINKS, H)
-        weave("vector", k_grouped[:, 4 * H : 12 * P], k_listed[:], H, 3 * P)
+        weave("vector", k_grouped[:, 4 * H : 4 * 416], k_listed[:], H, 416)
         q_codes, q_scales = planes("q", NQ)
         k_codes = tile([P, N], U32, "k_codes")
         k_scales = tile_at(AT_Q + 1024, [P, N], U8, "k_scales")
@@ -139,7 +139,7 @@ def tile_attend_ring_alibi_kernel(tc, qT, kT, vT, vs, pos, slope, offs, out):
             scores.append(bank)
 
         v_round = tile([P, T], BF16, "v_round")
-        for a, b in ((0, 256), (256, 512), (512, T)):
+        for a, b in ((0, 512), (512, T)):
             nc.scalar.activation(v_round[:, a:b], v_raw[0][:, a:b], COPY)
         v_listed0 = tile([P, N], BF16, "v_listed0")
         nc.scalar.activation(v_listed0[:], v_round[:].indirect(offsets[:]), COPY)

@@ -37,16 +37,16 @@ def tile_attend_ring_alibi_kernel(tc, qT, kT, vT, vs, pos, slope, offs, out):
         def tile_at(offset, shape, dtype, name):
             return reuse.tile(shape, dtype, name=name, align_bytes=64, offset=offset)
 
-        AT_B, AT_Q, AT_V, AT_R, AT_G = 0, 2048, 5120, 9216, 17408
+        AT_B, AT_Q, AT_V, AT_R, AT_G, AT_K = 0, 2048, 5120, 9216, 17408, 23040
         offsets = held.tile([P, N // 16], U16, name="offsets")
-        k_raw = [tile([P, T], F32, f"k_raw{t}") for t in range(4)]
+        k_pool = tile_at(AT_K, [P, 4 * T], F32, "k_pool")
         v_raw = [tile_at(AT_V, [P, T], F32, "v_raw0"), tile([P, T], F32, "v_raw1")]
         q_raw = tile_at(AT_Q, [P, 4, NQ], F32, "q_raw")
         pos_pool = tile_at(AT_R, [P, T], F32, "pos_pool")
         vs_pool = tile_at(AT_R + 4096, [P, T], F32, "vs_pool")
         slope_rows = tile([P, P], F32, "slope_rows")
 
-        k_rows = kT.rearrange("(p t) n -> p t n", t=4)
+        k_rows = kT.rearrange("(p t) n -> p (t n)", t=4)
 
         ident = tile([P, P], F32, "ident")
         make_identity(nc, ident[:])
@@ -54,14 +54,12 @@ def tile_attend_ring_alibi_kernel(tc, qT, kT, vT, vs, pos, slope, offs, out):
         nc.vector.memset(vs_pool[0:LAST, :], 0.0)
         nc.gpsimd.memset(slope_rows[0:LAST, :], 0.0)
         nc.sync.dma_start(offsets[:], offs)
-        nc.scalar.dma_start(out=k_raw[0][:], in_=k_rows[:, 0, :])
+        nc.scalar.dma_start(out=k_pool[:, 0:T], in_=k_rows[:, 0:T])
         nc.sync.dma_start(out=pos_pool[LAST:P, :], in_=pos[0:1, :])
         nc.sync.dma_start(out=vs_pool[LAST:P, :], in_=vs[0:1, :])
         nc.sync.dma_start(out=slope_rows[LAST:P, :], in_=slope[0].rearrange("q o -> o q"))
-        nc.sync.dma_start(out=k_raw[1][:], in_=k_rows[:, 1, :])
-        nc.sync.dma_start(out=k_raw[3][:, 0:HEAD], in_=k_rows[:, 3, 0:HEAD])
-        nc.sync.dma_start(out=k_raw[2][:], in_=k_rows[:, 2, :])
-        nc.sync.dma_start(out=k_raw[3][:, HEAD:T], in_=k_rows[:, 3, HEAD:T])
+        for a, b in ((T, 2 * T), (2 * T, 3 * T + HEAD), (3 * T + HEAD, 4 * T)):
+            nc.sync.dma_start(out=k_pool[:, a:b], in_=k_rows[:, a:b])
         nc.sync.dma_start(out=q_raw[:], in_=qT[0].rearrange("(p t) q -> p t q", t=4))
         for h in range(2):
             nc.sync.dma_start(out=v_raw[0][:, h * 512 : (h + 1) * 512], in_=vT[0:P, h * 512 : (h + 1) * 512])
@@ -96,7 +94,7 @@ def tile_attend_ring_alibi_kernel(tc, qT, kT, vT, vs, pos, slope, offs, out):
             nc.scalar.copy(pos_cols[h][:], pos_bank[:, :, LAST])
         slope_bank = psum.tile([P, P], F32, name="slope_bank", tag="v_bank")
         nc.tensor.transpose(slope_bank[:], slope_rows[:], ident[:])
-        slope_col = tile_at(AT_G + 4096 - 64, [P, 32], F32, "slope_col")[:, 0:1]
+        slope_col = tile_at(AT_G + 1024, [P, 1152], F32, "slope_col")[:, 0:1]
         nc.scalar.copy(slope_col, slope_bank[:, LAST:P])
         bias = tile_at(AT_B, [P, 4, P], F32, "bias")
         for h in range(2):
@@ -111,41 +109,48 @@ def tile_attend_ring_alibi_kernel(tc, qT, kT, vT, vs, pos, slope, offs, out):
         k_listed = tile_at(AT_R, [P, 4 * N], F32, "k_listed")
 
         def gather_keys(t, a, b, tokens):
-            nc.vector.tensor_copy(k_listed[:, t * N + a : t * N + b], k_raw[t][:, 0:tokens].indirect(offsets[:, a // 16 : b // 16]))
+            nc.vector.tensor_copy(k_listed[:, t * N + a : t * N + b], k_pool[:, t * T : t * T + tokens].indirect(offsets[:, a // 16 : b // 16]))
 
         gather_keys(0, 0, N, T)
         gather_keys(1, 0, N, T)
         gather_keys(3, 0, SINKS, HEAD)
         gather_keys(2, 0, N, T)
-        gather_keys(3, SINKS, H, T)
-        gather_keys(3, H, N, T)
-        k_grouped = tile_at(AT_G, [P, 4 * N], BF16, "k_grouped")
-        weave("scalar", k_grouped[:, 0 : 4 * SINKS], k_listed[:], 0, SINKS)
-        q_grouped = tile_at(AT_G + 4096, [P, 4 * NQ], BF16, "q_grouped")
-        weave("scalar", q_grouped[:], q_raw[:].rearrange("p t q -> p (t q)"), 0, NQ)
-        weave("scalar", k_grouped[:, 4 * 416 : 4 * N], k_listed[:], 416, N)
-        weave("vector", k_grouped[:, 4 * SINKS : 4 * H], k_listed[:], SINKS, H)
-        weave("vector", k_grouped[:, 4 * H : 4 * 416], k_listed[:], H, 416)
+        gather_keys(3, SINKS, 192, T)
+        gather_keys(3, 192, 320, T)
+        gather_keys(3, 320, N, T)
+        k_first = tile_at(AT_G + 1024, [P, 4 * P], BF16, "k_first")
+        k_rest = tile_at(AT_G + 2048, [P, 4 * (N - P)], BF16, "k_rest")
+        for a, b in ((0, SINKS), (SINKS, P)):
+            weave("scalar", k_first[:, 4 * a : 4 * b], k_listed[:], a, b)
+        for a, b in ((288, 384), (384, N)):
+            weave("scalar", k_rest[:, 4 * (a - P) : 4 * (b - P)], k_listed[:], a, b)
+        weave("vector", k_rest[:, 0 : 4 * (288 - P)], k_listed[:], P, 288)
+        k_grouped = [k_first[:]] + [k_rest[:, 4 * j * P : 4 * (j + 1) * P] for j in range(3)]
+        q_grouped = tile_at(AT_K - 512, [P, 4 * NQ], BF16, "q_grouped")
+        weave("vector", q_grouped[:], q_raw[:].rearrange("p t q -> p (t q)"), 0, NQ)
         q_codes, q_scales = planes("q", NQ)
         k_codes = tile([P, N], U32, "k_codes")
-        k_scales = tile_at(AT_Q + 1024, [P, N], U8, "k_scales")
-        nc.vector.quantize_mx(out=q_codes[:].bitcast(FP8X4), scales=q_scales[:], in_=q_grouped[:])
-        scores = []
-        for j in range(4):
+        k_scales_early = tile([P, P], U8, "k_scales_early")
+        k_scales_late = tile_at(AT_Q, [P, N], U8, "k_scales_late")
+        scores = {}
+        for j in (1, 0, 2, 3):
             cols = slice(j * P, (j + 1) * P)
-            nc.vector.quantize_mx(out=k_codes[:, cols].bitcast(FP8X4), scales=k_scales[:, cols], in_=k_grouped[:, 4 * j * P : 4 * (j + 1) * P])
+            k_scales = k_scales_early[:] if j == 1 else k_scales_late[:, cols]
+            nc.vector.quantize_mx(out=k_codes[:, cols].bitcast(FP8X4), scales=k_scales, in_=k_grouped[j])
+            if j == 1:
+                nc.vector.quantize_mx(out=q_codes[:].bitcast(FP8X4), scales=q_scales[:], in_=q_grouped[:])
             bank = psum.tile([P, P], F32, name=f"scores{j}", tag=f"scores{j}")
-            nc.tensor.matmul_mx(out=bank[:], lhsT=q_codes[:].bitcast(FP8X4), lhsT_scale=q_scales[:], rhs=k_codes[:, cols].bitcast(FP8X4), rhs_scale=k_scales[:, cols], start=True, stop=True)
-            scores.append(bank)
+            nc.tensor.matmul_mx(out=bank[:], lhsT=q_codes[:].bitcast(FP8X4), lhsT_scale=q_scales[:], rhs=k_codes[:, cols].bitcast(FP8X4), rhs_scale=k_scales, start=True, stop=True)
+            scores[j] = bank
 
-        v_round = tile([P, T], BF16, "v_round")
+        v_round = tile_at(AT_Q + 512, [P, T], BF16, "v_round")
         for a, b in ((0, 512), (512, T)):
             nc.scalar.activation(v_round[:, a:b], v_raw[0][:, a:b], COPY)
         v_listed0 = tile([P, N], BF16, "v_listed0")
         nc.scalar.activation(v_listed0[:], v_round[:].indirect(offsets[:]), COPY)
 
         s = tile_at(AT_R, [P, 4, P], F32, "s")
-        for j in range(4):
+        for j in (1, 0, 2, 3):
             part = slice(j * 32, (j + 1) * 32)
             nc.vector.tensor_tensor(s[:, :, part], scores[j][:].rearrange("p (i t) -> p t i", t=4), bias[:, :, part], ADD)
         minus_m = tile([P, 1], F32, "minus_m")

@@ -9,6 +9,7 @@ LAST = P - 1
 H = N // 2
 SINKS = 64
 HEAD = 256
+SPLIT = 320
 FLOPS = 2 * NQ * N * (D + DV)
 
 F32 = mybir.dt.float32
@@ -51,8 +52,8 @@ def tile_attend_ring_alibi_kernel(tc, qT, kT, vT, vs, pos, slope, offs, out):
         ident = tile([P, P], F32, "ident")
         make_identity(nc, ident[:])
         nc.vector.memset(pos_pool[0:LAST, :], 0.0)
-        nc.vector.memset(vs_pool[0:LAST, :], 0.0)
         nc.gpsimd.memset(slope_rows[0:LAST, :], 0.0)
+        nc.gpsimd.memset(vs_pool[0:LAST, :], 0.0)
         nc.sync.dma_start(offsets[:], offs)
         nc.scalar.dma_start(out=k_pool[:, 0:T], in_=k_rows[:, 0:T])
         nc.sync.dma_start(out=pos_pool[LAST:P, :], in_=pos[0:1, :])
@@ -122,9 +123,9 @@ def tile_attend_ring_alibi_kernel(tc, qT, kT, vT, vs, pos, slope, offs, out):
         k_rest = tile_at(AT_G + 2048, [P, 4 * (N - P)], BF16, "k_rest")
         for a, b in ((0, SINKS), (SINKS, P)):
             weave("scalar", k_first[:, 4 * a : 4 * b], k_listed[:], a, b)
-        for a, b in ((288, 384), (384, N)):
+        for a, b in ((SPLIT, 384), (384, N)):
             weave("scalar", k_rest[:, 4 * (a - P) : 4 * (b - P)], k_listed[:], a, b)
-        weave("vector", k_rest[:, 0 : 4 * (288 - P)], k_listed[:], P, 288)
+        weave("vector", k_rest[:, 0 : 4 * (SPLIT - P)], k_listed[:], P, SPLIT)
         k_grouped = [k_first[:]] + [k_rest[:, 4 * j * P : 4 * (j + 1) * P] for j in range(3)]
         q_grouped = tile_at(AT_K - 512, [P, 4 * NQ], BF16, "q_grouped")
         weave("vector", q_grouped[:], q_raw[:].rearrange("p t q -> p (t q)"), 0, NQ)
@@ -147,7 +148,7 @@ def tile_attend_ring_alibi_kernel(tc, qT, kT, vT, vs, pos, slope, offs, out):
         for a, b in ((0, 512), (512, T)):
             nc.scalar.activation(v_round[:, a:b], v_raw[0][:, a:b], COPY)
         v_listed0 = tile([P, N], BF16, "v_listed0")
-        nc.scalar.activation(v_listed0[:], v_round[:].indirect(offsets[:]), COPY)
+        nc.scalar.activation(v_listed0[:].rearrange("p (u s e) -> p s u e", u=2, e=2), v_round[:].indirect(offsets[:]), COPY)
 
         s = tile_at(AT_R, [P, 4, P], F32, "s")
         for j in (1, 0, 2, 3):
@@ -180,17 +181,20 @@ def tile_attend_ring_alibi_kernel(tc, qT, kT, vT, vs, pos, slope, offs, out):
 
         v_listed1 = tile_at(AT_B, [P, N], BF16, "v_listed1")
         nc.vector.tensor_copy(v_listed1[:].rearrange("p (u s e) -> p s u e", u=2, e=2), v_raw[1][:].indirect(offsets[:]))
-        v_grouped0 = turn_values(0, [v_listed0[:].bitcast(F32)[:, u : N // 2 : 2] for u in range(2)], tile_at(AT_B + 1024, [P, P, 4], BF16, "v_grouped0"))
+        v_grouped0 = turn_values(0, [v_listed0[:].bitcast(F32)[:, u * P : (u + 1) * P] for u in range(2)], tile_at(AT_B + 1024, [P, P, 4], BF16, "v_grouped0"))
         total = tile([P, 1], F32, "total")
         sums_again = tile([P, 4], F32, "sums_again")
         nc.scalar.activation(sums_again[:], sums[:], COPY, accum_out=total[:])
         nc.vector.quantize_mx(out=v_codes[:, 0:128].bitcast(FP8X4), scales=v_scales[:, 0:128], in_=v_grouped0[:].rearrange("p e t -> p (e t)"))
 
         w_grouped = tile([P, NQ, 4], BF16, "w_grouped")
-        nc.vector.tensor_tensor(w_grouped[:], p_bank[:].rearrange("p t q -> p q t"), vs_cols[:].unsqueeze(1).to_broadcast([P, NQ, 4]), MULT)
+        row_halves = (slice(0, NQ // 2), slice(NQ // 2, NQ))
+        for rows in row_halves:
+            nc.vector.tensor_tensor(w_grouped[:, rows, :], p_bank[:].rearrange("p t q -> p q t")[:, rows, :], vs_cols[:].unsqueeze(1).to_broadcast([P, NQ // 2, 4]), MULT)
         v_grouped1 = turn_values(1, [v_listed1[:].bitcast(F32)[:, u * P : (u + 1) * P] for u in range(2)], tile([P, P, 4], BF16, "v_grouped1"))
         w_codes, w_scales = planes("w", NQ)
-        nc.vector.quantize_mx(out=w_codes[:].bitcast(FP8X4), scales=w_scales[:], in_=w_grouped[:].rearrange("p q t -> p (q t)"))
+        for rows in row_halves:
+            nc.vector.quantize_mx(out=w_codes[:, rows].bitcast(FP8X4), scales=w_scales[:, rows], in_=w_grouped[:, rows, :].rearrange("p q t -> p (q t)"))
         nc.vector.quantize_mx(out=v_codes[:, 128:256].bitcast(FP8X4), scales=v_scales[:, 128:256], in_=v_grouped1[:].rearrange("p e t -> p (e t)"))
         inv = tile([P, 1], F32, "inv")
         nc.vector.reciprocal(inv[:], total[:])

@@ -66,11 +66,6 @@ def tile_attend_ring_alibi_kernel(tc, qT, kT, vT, vs, pos, slope, offs, out):
             nc.sync.dma_start(out=v_raw[0][:, h * 512 : (h + 1) * 512], in_=vT[0:P, h * 512 : (h + 1) * 512])
         nc.sync.dma_start(out=v_raw[1][:], in_=vT[P : 2 * P, :])
 
-        warm = tile([P, 1], F32, "warm")
-        warm_out = tile([P, 1], F32, "warm_out")
-        nc.vector.memset(warm[:], 0.0)
-        nc.scalar.activation(warm_out[:], warm[:], EXP)
-
         def planes(name, width):
             return tile([P, width], U32, name + "_codes"), tile([P, width], U8, name + "_scales")
 

@@ -6,6 +6,7 @@ from concourse.masks import make_identity
 NQ, D, N, T, DV = 128, 512, 512, 1024, 256
 P = 128
 LAST = P - 1
+MID = P // 2 - 1
 H = N // 2
 SINKS = 64
 HEAD = 256
@@ -53,11 +54,12 @@ def tile_attend_ring_alibi_kernel(tc, qT, kT, vT, vs, pos, slope, offs, out):
         make_identity(nc, ident[:])
         nc.vector.memset(pos_pool[0:LAST, :], 0.0)
         nc.gpsimd.memset(slope_rows[0:LAST, :], 0.0)
-        nc.gpsimd.memset(vs_pool[0:LAST, :], 0.0)
+        nc.vector.memset(vs_pool[0:MID, :], 0.0)
+        nc.gpsimd.memset(vs_pool[MID + 1 : P, :], 0.0)
         nc.sync.dma_start(offsets[:], offs)
         nc.scalar.dma_start(out=k_pool[:, 0:T], in_=k_rows[:, 0:T])
         nc.sync.dma_start(out=pos_pool[LAST:P, :], in_=pos[0:1, :])
-        nc.sync.dma_start(out=vs_pool[LAST:P, :], in_=vs[0:1, :])
+        nc.sync.dma_start(out=vs_pool[MID : MID + 1, :], in_=vs[0:1, :])
         nc.sync.dma_start(out=slope_rows[LAST:P, :], in_=slope[0].rearrange("q o -> o q"))
         for a, b in ((T, 2 * T), (2 * T, 3 * T + HEAD), (3 * T + HEAD, 4 * T)):
             nc.sync.dma_start(out=k_pool[:, a:b], in_=k_rows[:, a:b])
@@ -159,7 +161,7 @@ def tile_attend_ring_alibi_kernel(tc, qT, kT, vT, vs, pos, slope, offs, out):
             nc.scalar.activation(p[:, t * P : (t + 1) * P], s[:, t, :], EXP, bias=minus_m[:], accum_out=sums[:, t : t + 1])
             nc.tensor.transpose(p_bank[:, t, :], p[:, t * P : (t + 1) * P], ident[:])
         vs_cols = tile_at(AT_R, [P, 4], F32, "vs_cols")
-        nc.scalar.copy(vs_cols[:], vs_bank[:, :, LAST])
+        nc.scalar.copy(vs_cols[:], vs_bank[:, :, MID])
 
         v_codes, v_scales = planes("v", DV)
 

@@ -10,7 +10,8 @@ MID = P // 2 - 1
 H = N // 2
 SINKS = 64
 HEAD = 256
-SPLIT = 320
+SPLIT = 288
+PIECES = ((0, 128), (128, 256), (256, 384), (384, 448), (448, 512))
 FLOPS = 2 * NQ * N * (D + DV)
 
 F32 = mybir.dt.float32
@@ -81,8 +82,8 @@ def tile_attend_ring_alibi_kernel(tc, qT, kT, vT, vs, pos, slope, offs, out):
 
         pos_listed = tile([P, N], F32, "pos_listed")
         nc.vector.tensor_copy(pos_listed[:], pos_pool[:].indirect(offsets[:]))
-        vs_dealt = tile([P, 4, P], U32, "vs_dealt")
-        nc.vector.tensor_copy(vs_dealt[:].rearrange("p t s -> p s t"), vs_pool[:].bitcast(U32).indirect(offsets[:]))
+        vs_listed = tile([P, P, 4], F32, "vs_listed")
+        nc.vector.tensor_copy(vs_listed[:].rearrange("p s t -> p (s t)"), vs_pool[:].indirect(offsets[:]))
         pos_cols = []
         for h in range(2):
             pos_bank = psum.tile([P, 2, P], F32, name=f"pos_bank{h}", tag=("scores1", "vs_bank")[h])
@@ -102,7 +103,7 @@ def tile_attend_ring_alibi_kernel(tc, qT, kT, vT, vs, pos, slope, offs, out):
             nc.scalar.activation(bias[:, :, h * 64 : (h + 1) * 64], spread[:].rearrange("p (i t) -> p t i", t=4), COPY, scale=slope_col)
         vs_bank = psum.tile([P, 4, P], F32, name="vs_bank", tag="vs_bank")
         for t in range(4):
-            nc.tensor.transpose(vs_bank[:, t, :], vs_dealt[:, t, :].bitcast(F32), ident[:])
+            nc.tensor.transpose(vs_bank[:, t, :], vs_listed[:, :, t], ident[:])
 
         k_listed = tile_at(AT_R, [P, 4 * N], F32, "k_listed")
 
@@ -120,10 +121,10 @@ def tile_attend_ring_alibi_kernel(tc, qT, kT, vT, vs, pos, slope, offs, out):
         k_rest = tile_at(AT_G + 2048, [P, 4 * (N - P)], BF16, "k_rest")
         for a, b in ((0, SINKS), (SINKS, P)):
             weave("scalar", k_first[:, 4 * a : 4 * b], k_listed[:], a, b)
-        for a, b in ((SPLIT, 384), (384, N)):
+        for a, b in ((SPLIT, 320), (320, 384), (384, 448), (448, N)):
             weave("scalar", k_rest[:, 4 * (a - P) : 4 * (b - P)], k_listed[:], a, b)
         weave("vector", k_rest[:, 0 : 4 * (SPLIT - P)], k_listed[:], P, SPLIT)
-        k_grouped = [k_first[:]] + [k_rest[:, 4 * j * P : 4 * (j + 1) * P] for j in range(3)]
+        k_grouped = [k_first[:]] + [k_rest[:, 4 * (a - P) : 4 * (b - P)] for a, b in PIECES[1:]]
         q_grouped = tile_at(AT_K - 512, [P, 4 * NQ], BF16, "q_grouped")
         weave("vector", q_grouped[:], q_raw[:].rearrange("p t q -> p (t q)"), 0, NQ)
         q_codes, q_scales = planes("q", NQ)
@@ -131,13 +132,13 @@ def tile_attend_ring_alibi_kernel(tc, qT, kT, vT, vs, pos, slope, offs, out):
         k_scales_early = tile([P, P], U8, "k_scales_early")
         k_scales_late = tile_at(AT_Q, [P, N], U8, "k_scales_late")
         scores = {}
-        for j in (1, 0, 2, 3):
-            cols = slice(j * P, (j + 1) * P)
+        for j in (1, 0, 2, 3, 4):
+            cols = slice(*PIECES[j])
             k_scales = k_scales_early[:] if j == 1 else k_scales_late[:, cols]
             nc.vector.quantize_mx(out=k_codes[:, cols].bitcast(FP8X4), scales=k_scales, in_=k_grouped[j])
             if j == 1:
                 nc.vector.quantize_mx(out=q_codes[:].bitcast(FP8X4), scales=q_scales[:], in_=q_grouped[:])
-            bank = psum.tile([P, P], F32, name=f"scores{j}", tag=f"scores{j}")
+            bank = psum.tile([P, PIECES[j][1] - PIECES[j][0]], F32, name=f"scores{j}", tag=f"scores{j}" if j < 4 else "p0")
             nc.tensor.matmul_mx(out=bank[:], lhsT=q_codes[:].bitcast(FP8X4), lhsT_scale=q_scales[:], rhs=k_codes[:, cols].bitcast(FP8X4), rhs_scale=k_scales, start=True, stop=True)
             scores[j] = bank
 
@@ -148,8 +149,8 @@ def tile_attend_ring_alibi_kernel(tc, qT, kT, vT, vs, pos, slope, offs, out):
         nc.scalar.activation(v_listed0[:].rearrange("p (u s e) -> p s u e", u=2, e=2), v_round[:].indirect(offsets[:]), COPY)
 
         s = tile_at(AT_R, [P, 4, P], F32, "s")
-        for j in (1, 0, 2, 3):
-            part = slice(j * 32, (j + 1) * 32)
+        for j in (1, 0, 2, 3, 4):
+            part = slice(PIECES[j][0] // 4, PIECES[j][1] // 4)
             nc.vector.tensor_tensor(s[:, :, part], scores[j][:].rearrange("p (i t) -> p t i", t=4), bias[:, :, part], ADD)
         minus_m = tile([P, 1], F32, "minus_m")
         nc.vector.tensor_reduce(out=minus_m[:], in_=s[:].rearrange("p t i -> p (t i)"), axis=X, op=MAX, negate=True)

@@ -114,14 +114,13 @@ def tile_attend_ring_alibi_kernel(tc, qT, kT, vT, vs, pos, slope, offs, out):
         gather_keys(1, 0, N, T)
         gather_keys(3, 0, SINKS, HEAD)
         gather_keys(2, 0, N, T)
-        gather_keys(3, SINKS, 192, T)
-        gather_keys(3, 192, 320, T)
-        gather_keys(3, 320, N, T)
+        gather_keys(3, SINKS, SPLIT, T)
+        gather_keys(3, SPLIT, N, T)
         k_first = tile_at(AT_G + 1024, [P, 4 * P], BF16, "k_first")
         k_rest = tile_at(AT_G + 2048, [P, 4 * (N - P)], BF16, "k_rest")
         for a, b in ((0, SINKS), (SINKS, P)):
             weave("scalar", k_first[:, 4 * a : 4 * b], k_listed[:], a, b)
-        for a, b in ((SPLIT, 320), (320, 384), (384, 448), (448, N)):
+        for a, b in ((SPLIT, 384), (384, 448), (448, N)):
             weave("scalar", k_rest[:, 4 * (a - P) : 4 * (b - P)], k_listed[:], a, b)
         weave("vector", k_rest[:, 0 : 4 * (SPLIT - P)], k_listed[:], P, SPLIT)
         k_grouped = [k_first[:]] + [k_rest[:, 4 * (a - P) : 4 * (b - P)] for a, b in PIECES[1:]]

from contextlib import ExitStack

import concourse.mybir as mybir
from concourse.masks import make_identity

NQ, D, N, T, DV = 128, 512, 512, 1024, 256
P = 128
LAST = P - 1
MID = P // 2 - 1
H = N // 2
SINKS = 64
HEAD = 256
SPLIT = 288
PIECES = ((0, 128), (128, 256), (256, 384), (384, 448), (448, 512))
FLOPS = 2 * NQ * N * (D + DV)

F32 = mybir.dt.float32
BF16 = mybir.dt.bfloat16
U32 = mybir.dt.uint32
U16 = mybir.dt.uint16
U8 = mybir.dt.uint8
FP8X4 = mybir.dt.float8_e4m3fn_x4
ADD, MULT, MAX = mybir.AluOpType.add, mybir.AluOpType.mult, mybir.AluOpType.max
EXP = mybir.ActivationFunctionType.Exp
COPY = mybir.ActivationFunctionType.Copy
IDENTITY = mybir.ActivationFunctionType.Identity
X = mybir.AxisListType.X


def tile_attend_ring_alibi_kernel(tc, qT, kT, vT, vs, pos, slope, offs, out):
    nc = tc.nc
    with ExitStack() as ctx:
        held = ctx.enter_context(tc.tile_pool(name="held", bufs=1))
        reuse = ctx.enter_context(tc.tile_pool(name="reuse", bufs=1))
        psum = ctx.enter_context(tc.psum_pool(name="psum", bufs=1))

        def tile(shape, dtype, name, tag=None):
            return held.tile(shape, dtype, name=name, tag=tag or name, align_bytes=64)

        def tile_at(offset, shape, dtype, name):
            return reuse.tile(shape, dtype, name=name, align_bytes=64, offset=offset)

        AT_B, AT_Q, AT_V, AT_R, AT_G, AT_K = 0, 2048, 5120, 9216, 17408, 23040
        offsets = held.tile([P, N // 16], U16, name="offsets")
        k_pool = tile_at(AT_K, [P, 4 * T], F32, "k_pool")
        v_raw = [tile_at(AT_V, [P, T], F32, "v_raw0"), tile([P, T], F32, "v_raw1")]
        q_raw = tile_at(AT_Q, [P, 4, NQ], F32, "q_raw")
        pos_pool = tile_at(AT_R, [P, T], F32, "pos_pool")
        vs_pool = tile_at(AT_R + 4096, [P, T], F32, "vs_pool")
        slope_rows = tile([P, P], F32, "slope_rows")

        k_rows = kT.rearrange("(p t) n -> p (t n)", t=4)

        ident = tile([P, P], F32, "ident")
        make_identity(nc, ident[:])
        nc.vector.memset(pos_pool[0:LAST, :], 0.0)
        nc.gpsimd.memset(slope_rows[0:LAST, :], 0.0)
        nc.vector.memset(vs_pool[0:MID, :], 0.0)
        nc.gpsimd.memset(vs_pool[MID + 1 : P, :], 0.0)
        nc.sync.dma_start(offsets[:], offs)
        nc.scalar.dma_start(out=k_pool[:, 0:T], in_=k_rows[:, 0:T])
        nc.sync.dma_start(out=pos_pool[LAST:P, :], in_=pos[0:1, :])
        nc.sync.dma_start(out=vs_pool[MID : MID + 1, :], in_=vs[0:1, :])
        nc.sync.dma_start(out=slope_rows[LAST:P, :], in_=slope[0].rearrange("q o -> o q"))
        for a, b in ((T, 2 * T), (2 * T, 3 * T + HEAD), (3 * T + HEAD, 4 * T)):
            nc.sync.dma_start(out=k_pool[:, a:b], in_=k_rows[:, a:b])
        nc.sync.dma_start(out=q_raw[:], in_=qT[0].rearrange("(p t) q -> p t q", t=4))
        for h in range(2):
            nc.sync.dma_start(out=v_raw[0][:, h * 512 : (h + 1) * 512], in_=vT[0:P, h * 512 : (h + 1) * 512])
        nc.sync.dma_start(out=v_raw[1][:], in_=vT[P : 2 * P, :])

        def planes(name, width):
            return tile([P, width], U32, name + "_codes"), tile([P, width], U8, name + "_scales")

        def weave(engine, grouped, flat, a, b):
            dst = grouped.rearrange("p (c i t) -> p c t i", i=4, t=4)
            src = flat.rearrange("p (t c i) -> p c t i", t=4, i=4)[:, a // 4 : b // 4, :, :]
            if engine == "scalar":
                nc.scalar.activation(dst, src, COPY)
            else:
                nc.vector.tensor_copy(out=dst, in_=src)

        pos_listed = tile([P, N], F32, "pos_listed")
        nc.vector.tensor_copy(pos_listed[:], pos_pool[:].indirect(offsets[:]))
        vs_listed = tile([P, P, 4], F32, "vs_listed")
        nc.vector.tensor_copy(vs_listed[:].rearrange("p s t -> p (s t)"), vs_pool[:].indirect(offsets[:]))
        pos_cols = []
        for h in range(2):
            pos_bank = psum.tile([P, 2, P], F32, name=f"pos_bank{h}", tag=("scores1", "vs_bank")[h])
            for j in range(2):
                nc.tensor.transpose(pos_bank[:, j, :], pos_listed[:, (2 * h + j) * P : (2 * h + j + 1) * P], ident[:])
            pos_cols.append(tile([P, 2], F32, f"pos_cols{h}"))
            nc.scalar.copy(pos_cols[h][:], pos_bank[:, :, LAST])
        slope_bank = psum.tile([P, P], F32, name="slope_bank", tag="v_bank")
        nc.tensor.transpose(slope_bank[:], slope_rows[:], ident[:])
        slope_col = tile_at(AT_G + 1024, [P, 1152], F32, "slope_col")[:, 0:1]
        nc.scalar.copy(slope_col, slope_bank[:, LAST:P])
        bias = tile_at(AT_B, [P, 4, P], F32, "bias")
        for h in range(2):
            spread = psum.tile([P, H], F32, name=f"spread{h}", tag=("scores2", "y0")[h])
            for j in range(2):
                nc.tensor.transpose(spread[:, j * P : (j + 1) * P], pos_cols[h][:, j : j + 1].to_broadcast([P, P]), ident[:])
            nc.scalar.activation(bias[:, :, h * 64 : (h + 1) * 64], spread[:].rearrange("p (i t) -> p t i", t=4), COPY, scale=slope_col)
        vs_bank = psum.tile([P, 4, P], F32, name="vs_bank", tag="vs_bank")
        for t in range(4):
            nc.tensor.transpose(vs_bank[:, t, :], vs_listed[:, :, t], ident[:])

        k_listed = tile_at(AT_R, [P, 4 * N], F32, "k_listed")

        def gather_keys(t, a, b, tokens):
            nc.vector.tensor_copy(k_listed[:, t * N + a : t * N + b], k_pool[:, t * T : t * T + tokens].indirect(offsets[:, a // 16 : b // 16]))

        gather_keys(0, 0, N, T)
        gather_keys(1, 0, N, T)
        gather_keys(3, 0, SINKS, HEAD)
        gather_keys(2, 0, N, T)
        gather_keys(3, SINKS, SPLIT, T)
        gather_keys(3, SPLIT, N, T)
        k_first = tile_at(AT_G + 1024, [P, 4 * P], BF16, "k_first")
        k_rest = tile_at(AT_G + 2048, [P, 4 * (N - P)], BF16, "k_rest")
        for a, b in ((0, SINKS), (SINKS, P)):
            weave("scalar", k_first[:, 4 * a : 4 * b], k_listed[:], a, b)
        for a, b in ((SPLIT, 384), (384, 448), (448, N)):
            weave("scalar", k_rest[:, 4 * (a - P) : 4 * (b - P)], k_listed[:], a, b)
        weave("vector", k_rest[:, 0 : 4 * (SPLIT - P)], k_listed[:], P, SPLIT)
        k_grouped = [k_first[:]] + [k_rest[:, 4 * (a - P) : 4 * (b - P)] for a, b in PIECES[1:]]
        q_grouped = tile_at(AT_K - 512, [P, 4 * NQ], BF16, "q_grouped")
        weave("vector", q_grouped[:], q_raw[:].rearrange("p t q -> p (t q)"), 0, NQ)
        q_codes, q_scales = planes("q", NQ)
        k_codes = tile([P, N], U32, "k_codes")
        k_scales_early = tile([P, P], U8, "k_scales_early")
        k_scales_late = tile_at(AT_Q, [P, N], U8, "k_scales_late")
        scores = {}
        for j in (1, 0, 2, 3, 4):
            cols = slice(*PIECES[j])
            k_scales = k_scales_early[:] if j == 1 else k_scales_late[:, cols]
            nc.vector.quantize_mx(out=k_codes[:, cols].bitcast(FP8X4), scales=k_scales, in_=k_grouped[j])
            if j == 1:
                nc.vector.quantize_mx(out=q_codes[:].bitcast(FP8X4), scales=q_scales[:], in_=q_grouped[:])
            bank = psum.tile([P, PIECES[j][1] - PIECES[j][0]], F32, name=f"scores{j}", tag=f"scores{j}" if j < 4 else "p0")
            nc.tensor.matmul_mx(out=bank[:], lhsT=q_codes[:].bitcast(FP8X4), lhsT_scale=q_scales[:], rhs=k_codes[:, cols].bitcast(FP8X4), rhs_scale=k_scales, start=True, stop=True)
            scores[j] = bank

        v_round = tile_at(AT_Q + 512, [P, T], BF16, "v_round")
        for a, b in ((0, 512), (512, T)):
            nc.scalar.activation(v_round[:, a:b], v_raw[0][:, a:b], COPY)
        v_listed0 = tile([P, N], BF16, "v_listed0")
        nc.scalar.activation(v_listed0[:].rearrange("p (u s e) -> p s u e", u=2, e=2), v_round[:].indirect(offsets[:]), COPY)

        s = tile_at(AT_R, [P, 4, P], F32, "s")
        for j in (1, 0, 2, 3, 4):
            part = slice(PIECES[j][0] // 4, PIECES[j][1] // 4)
            nc.vector.tensor_tensor(s[:, :, part], scores[j][:].rearrange("p (i t) -> p t i", t=4), bias[:, :, part], ADD)
        minus_m = tile([P, 1], F32, "minus_m")
        nc.vector.tensor_reduce(out=minus_m[:], in_=s[:].rearrange("p t i -> p (t i)"), axis=X, op=MAX, negate=True)

        p_bank = psum.tile([P, 4, P], F32, name="p_bank", tag="p0")
        sums = tile([P, 4], F32, "sums")
        p = tile_at(AT_V, [P, 4 * P], F32, "p")
        for t in range(4):
            nc.scalar.activation(p[:, t * P : (t + 1) * P], s[:, t, :], EXP, bias=minus_m[:], accum_out=sums[:, t : t + 1])
            nc.tensor.transpose(p_bank[:, t, :], p[:, t * P : (t + 1) * P], ident[:])
        vs_cols = tile_at(AT_R, [P, 4], F32, "vs_cols")
        nc.scalar.copy(vs_cols[:], vs_bank[:, :, MID])

        v_codes, v_scales = planes("v", DV)

        def turn_values(j, halves, grouped):
            bank = psum.tile([P, 2, P], F32, name=f"v_bank{j}", tag="v_bank" if j == 0 else "vs_bank")
            for u in range(2):
                nc.tensor.transpose(bank[:, u, :], halves[u], ident[:])
            words = grouped[:].rearrange("p e t -> p (e t)").bitcast(F32).rearrange("p (e u) -> p e u", u=2)
            if j == 0:
                nc.vector.tensor_copy(words, bank[:].rearrange("p u e -> p e u"))
            else:
                nc.scalar.copy(words, bank[:].rearrange("p u e -> p e u"))
            return grouped

        v_listed1 = tile_at(AT_B, [P, N], BF16, "v_listed1")
        nc.vector.tensor_copy(v_listed1[:].rearrange("p (u s e) -> p s u e", u=2, e=2), v_raw[1][:].indirect(offsets[:]))
        v_grouped0 = turn_values(0, [v_listed0[:].bitcast(F32)[:, u * P : (u + 1) * P] for u in range(2)], tile_at(AT_B + 1024, [P, P, 4], BF16, "v_grouped0"))
        total = tile([P, 1], F32, "total")
        sums_again = tile([P, 4], F32, "sums_again")
        nc.scalar.activation(sums_again[:], sums[:], COPY, accum_out=total[:])
        nc.vector.quantize_mx(out=v_codes[:, 0:128].bitcast(FP8X4), scales=v_scales[:, 0:128], in_=v_grouped0[:].rearrange("p e t -> p (e t)"))

        w_grouped = tile([P, NQ, 4], BF16, "w_grouped")
        row_halves = (slice(0, NQ // 2), slice(NQ // 2, NQ))
        for rows in row_halves:
            nc.vector.tensor_tensor(w_grouped[:, rows, :], p_bank[:].rearrange("p t q -> p q t")[:, rows, :], vs_cols[:].unsqueeze(1).to_broadcast([P, NQ // 2, 4]), MULT)
        v_grouped1 = turn_values(1, [v_listed1[:].bitcast(F32)[:, u * P : (u + 1) * P] for u in range(2)], tile([P, P, 4], BF16, "v_grouped1"))
        w_codes, w_scales = planes("w", NQ)
        for rows in row_halves:
            nc.vector.quantize_mx(out=w_codes[:, rows].bitcast(FP8X4), scales=w_scales[:, rows], in_=w_grouped[:, rows, :].rearrange("p q t -> p (q t)"))
        nc.vector.quantize_mx(out=v_codes[:, 128:256].bitcast(FP8X4), scales=v_scales[:, 128:256], in_=v_grouped1[:].rearrange("p e t -> p (e t)"))
        inv = tile([P, 1], F32, "inv")
        nc.vector.reciprocal(inv[:], total[:])

        HV = DV // 2
        for h in range(2):
            cols = slice(h * HV, (h + 1) * HV)
            y = psum.tile([P, HV], F32, name=f"y{h}", tag="y0" if h == 0 else "scores0")
            nc.tensor.matmul_mx(out=y[:], lhsT=w_codes[:].bitcast(FP8X4), lhsT_scale=w_scales[:], rhs=v_codes[:, cols].bitcast(FP8X4), rhs_scale=v_scales[:, cols], start=True, stop=True)
            res = tile([P, HV], F32, f"res{h}")
            if h == 0:
                nc.scalar.activation(res[:], y[:], COPY, scale=inv[:])
            else:
                nc.vector.tensor_scalar(res[:], y[:], inv[:], None, MULT)
            nc.sync.dma_start(out=out[0][:, cols], in_=res[:])
